import numpy as np
import ml_dtypes


def mxq(x, axis, fmt="e4m3"):
    dtype, down = {"e4m3": (ml_dtypes.float8_e4m3fn, 7), "e5m2": (ml_dtypes.float8_e5m2, 14)}[fmt]
    v = np.moveaxis(np.asarray(x, np.float32).astype(ml_dtypes.bfloat16).astype(np.float64), axis, -1)
    blocks = v.reshape(v.shape[:-1] + (-1, 32))
    amax = np.abs(blocks).max(-1, keepdims=True)
    byte = np.maximum(np.where(amax > 0, np.frexp(amax)[1] - 1 + 127, 0) - down, 1)
    scale = np.exp2(byte - 127.0)
    codes = (blocks / scale).astype(np.float32).astype(dtype).astype(np.float64)
    return np.moveaxis((codes * scale).reshape(v.shape), -1, axis)


WIDE = False


def mx_kscale(k):
    if not WIDE:
        return np.ones(k)
    levels = np.array([10, -10, 5, -5, 0])
    if k % 512:
        return np.exp2(np.random.permutation(np.resize(levels, k // 32))).repeat(32)
    a = np.empty((k // 512, 16))
    for p in range(k // 512):
        a[p, :8] = np.random.permutation(np.resize(levels, 8))
        for g in range(8):
            far = levels[np.abs(levels - a[p, g]) >= 10]
            a[p, g + 8] = far[np.random.randint(len(far))]
    return np.exp2(a.ravel()).repeat(32)


def f64(x):
    return np.asarray(x).astype(np.float64)


def striped(idx):
    return np.tile(idx.reshape(-1, 16).T, (8, 1)).astype(np.uint16)


def unstriped(offs):
    return offs[:16].T.reshape(-1).astype(np.int64)


E2M1 = np.array([0.0, 0.5, 1.0, 1.5, 2.0, 3.0, 4.0, 6.0, -0.0, -0.5, -1.0, -1.5, -2.0, -3.0, -4.0, -6.0])


def pack_weight(w, fmt):
    k, n = w.shape
    w = f64(np.asarray(w, np.float32).astype(ml_dtypes.bfloat16)).reshape(k // 32, 32, n)
    amax = np.abs(w).max(1)
    if fmt == "e4m3":
        byte = np.frexp(amax)[1] - 1 + 127 - 7
    else:
        mant, ex = np.frexp(amax / 6.0)
        byte = np.where(mant > 0.5, ex, ex - 1) + 127
    byte = np.clip(np.where(amax > 0, byte, 1), 1, 254)
    scaled = (w * np.exp2(127.0 - byte)[:, None, :]).reshape(k, n).astype(np.float32)
    by_word = np.ascontiguousarray(scaled.reshape(k // 512, 128, 4, n).transpose(0, 1, 3, 2))
    if fmt == "e4m3":
        words = by_word.astype(ml_dtypes.float8_e4m3fn).view(np.uint8)
    else:
        c = by_word.astype(ml_dtypes.float4_e2m1fn).view(np.uint8) & 0xF
        words = (c[..., 0::2] | (c[..., 1::2] << 4)).reshape(k // 512, 128, 2 * n)
    return np.ascontiguousarray(words), np.ascontiguousarray(byte.astype(np.uint8).reshape(k // 512, 16, n))


def unpack_weight(words, scales, fmt):
    g, _, n = scales.shape
    words = np.ascontiguousarray(words).reshape(g, 128, n, -1)
    if fmt == "e4m3":
        vals = words.view(ml_dtypes.float8_e4m3fn).astype(np.float64)
    else:
        nib = np.empty((g, 128, n, 4), np.uint8)
        nib[..., 0::2] = words & 0xF
        nib[..., 1::2] = words >> 4
        vals = E2M1[nib]
    vals = vals * np.repeat(np.exp2(scales.astype(np.float64) - 127.0), 8, axis=1)[..., None]
    return vals.transpose(0, 1, 3, 2).reshape(g * 512, n)


def gelu(v):
    return 0.5 * v * (1.0 + np.tanh(np.sqrt(2.0 / np.pi) * (v + 0.044715 * v**3)))


K, H, N, T, S, T2, P = 1536, 1024, 384, 4096, 1024, 2048, 1024

def setup_inputs():
    n = np.random.standard_normal
    s = mx_kscale(K)[:, None]
    u = mx_kscale(H)[:, None]
    tab_words, tab_scales = pack_weight(n((K, T)) * s, "e4m3")
    w4_words, w4_scales = pack_weight(n((H, N)) / np.sqrt(H) / u, "e2m1")
    return {
        "tab_words": tab_words, "tab_scales": tab_scales,
        "offs": striped(np.random.permutation(T)[:S]),
        "w1": (0.6 * n((K, H)) / np.sqrt(K) / s).astype(np.float32),
        "centre": (0.6 * n(H)).astype(np.float32),
        "offs2": striped(np.random.permutation(T2)[:S]),
        "wgs": np.exp(0.3 * n((128, S))).astype(np.float32),
        "bedw": (n((H, T2)) * u).astype(np.float32),
        "w4_words": w4_words, "w4_scales": w4_scales,
        "offs3": striped(np.random.permutation(T2)[:P]),
        "offs4": striped(np.random.permutation(T2)[:P]),
        "wgo": np.exp(0.3 * n((128, P))).astype(np.float32),
    }

def reference(tab_words, tab_scales, offs, w1, centre, offs2, wgs, bedw,
              w4_words, w4_scales, offs3, offs4, wgo):
    v = unpack_weight(tab_words, tab_scales, "e4m3")[:, unstriped(offs)]
    a = mxq(f64(w1), 0, "e4m3").T @ v
    h = np.square(a - f64(centre)[:, None])
    page = np.zeros((H, T2))
    page[:, unstriped(offs2)] = np.tile(f64(wgs), (H // 128, 1)) * h
    z = np.exp(-page) * f64(bedw)
    w4 = unpack_weight(w4_words, w4_scales, "e2m1")
    y = w4.T @ mxq(z, 0, "e4m3")
    x = y[:, unstriped(offs3)]
    x = np.log1p(np.square(x))
    out = np.zeros((N, T2))
    out[:, unstriped(offs4)] = np.tile(f64(wgo), (N // 128, 1)) * x
    return out

@@ -1,0 +1,265 @@
+from contextlib import ExitStack
+
+import concourse.mybir as mybir
+
+K, H, N, T, S, T2, PK = 1536, 1024, 384, 4096, 1024, 2048, 1024
+FLOPS = 2 * K * H * S + 2 * H * N * T2
+
+F32 = mybir.dt.float32
+BF16 = mybir.dt.bfloat16
+I32 = mybir.dt.int32
+U32 = mybir.dt.uint32
+U16 = mybir.dt.uint16
+U8 = mybir.dt.uint8
+FP8X4 = mybir.dt.float8_e4m3fn_x4
+FP4X4 = mybir.dt.float4_e2m1fn_x4
+ACT = mybir.ActivationFunctionType
+MULT = mybir.AluOpType.mult
+
+P = 128
+KP = 512
+PASS1 = K // KP
+PASS2 = H // KP
+NT = N // P
+BANK = 512
+PAGES = 3
+OUTS = 2
+QUADS = (0, 2, 1, 3)
+CHUNKS0 = [(0, 512), (512, 512), (1024, 512), (1536, 512)]
+CHUNKS1 = [(0, 128), (128, 128), (256, 256), (512, 512), (1024, 512), (1536, 256), (1792, 128), (1920, 128)]
+
+
+def tile_list_bed_request_matching_kernel(
+    tc, tab_words, tab_scales, offs, w1, centre, offs2, wgs, bedw,
+    w4_words, w4_scales, offs3, offs4, wgo, out,
+):
+    nc = tc.nc
+    with ExitStack() as ctx:
+        lists = ctx.enter_context(tc.tile_pool(name="lists", bufs=1))
+        keep = ctx.enter_context(tc.tile_pool(name="keep", bufs=1))
+        psum = ctx.enter_context(tc.psum_pool(name="psum", bufs=4))
+
+        def sb(shape, dtype, name, tag=None, bufs=1):
+            return keep.tile(shape, dtype, name=name, tag=tag or name, bufs=bufs, align_bytes=64)
+
+        def load_list(src, name):
+            tile = lists.tile([P, S // 16], U16, name=name)
+            nc.sync.dma_start(tile[:], src)
+            return tile
+
+        def load_table(a):
+            tile = sb([P, T], I32, "tab%d" % a, tag=("big0", "big1", "close")[a])
+            nc.sync.dma_start(tile[:], tab_words[a].rearrange("p t i -> p (t i)").bitcast(I32))
+            return tile
+
+        def load_w1(dst, a, b):
+            rows = w1[a * KP:(a + 1) * KP, b * KP:(b + 1) * KP]
+            nc.sync.dma_start(dst, rows.rearrange("(p j) c -> p j c", j=4))
+
+        def load_wgs(t0, t1):
+            tile = sb([P, t1 - t0, S], F32, "wgs%d" % t0)
+            src = wgs.rearrange("(q t) j -> q t j", t=4)[:, t0:t1, :]
+            for q in QUADS:
+                nc.sync.dma_start(tile[32 * q:32 * q + 32, :, :], src)
+            return [tile[:, i, :] for i in range(t1 - t0)]
+
+        def load_bed(b, half, slot):
+            tile = sb([P, 4, T2 // 2], F32, "bed%d%d" % (b, half), tag="big%d" % slot)
+            cols = slice(half * (T2 // 2), (half + 1) * (T2 // 2))
+            nc.sync.dma_start(tile[:], bedw[b * KP:(b + 1) * KP, cols].rearrange("(p t) c -> p t c", t=4))
+            return tile
+
+        def staging(name):
+            return sb([P, 4 * KP], BF16, name, tag="stage", bufs=3)
+
+        tab_sc = sb([P, T], U8, "tab_sc", tag="h", bufs=3)
+        nc.vector.memset(tab_sc[:].bitcast(I32), 0)
+        for q in QUADS:
+            nc.gpsimd.dma_start(
+                tab_sc[32 * q:32 * q + 4 * PASS1, :].bitcast(I32),
+                tab_scales[:, 4 * q:4 * q + 4, :].bitcast(I32),
+            )
+        w4_sc = sb([P, PASS2, N], U8, "w4_sc")
+        nc.vector.memset(w4_sc[:].rearrange("p a c -> p (a c)").bitcast(I32), 0)
+        pages = [sb([P, T2], F32, "page%d" % i) for i in range(PAGES)]
+        outs = [sb([P, T2], F32, "desk%d" % i) for i in range(OUTS)]
+        for tile in pages + outs:
+            nc.vector.memset(tile[:], 0.0)
+
+        idx1 = load_list(offs, "idx1")
+        idx2 = load_list(offs2, "idx2")
+        cen = sb([P, PASS2, 4], F32, "cen")
+        nc.sync.dma_start(cen[:], centre.rearrange("(b p t) -> p b t", b=PASS2, t=4))
+        raw0 = [sb([P, 4, KP], F32, "raw0_%d" % a, tag="y%d" % a) for a in range(PASS1)]
+        tabs = [load_table(0)]
+        for a in range(PASS1):
+            load_w1(raw0[a][:], a, 0)
+        tabs.extend([load_table(a) for a in range(1, PASS1)])
+        wgs_sb = load_wgs(0, 1)
+        wgs_sb.extend(load_wgs(1, 2))
+        wgs_sb.extend(load_wgs(2, 4))
+
+        v_codes = [sb([P, S], U32, "v_codes%d" % a) for a in range(PASS1)]
+        v_sc = sb([P, S], U8, "v_sc")
+        w_codes = [[sb([P, KP], U32, "w_codes0%d" % a)[:] for a in range(PASS1)]]
+        w_sc = [[sb([P, KP], U8, "w_sc%d%d" % (b, a)) for a in range(PASS1)] for b in range(PASS2)]
+
+        def round_w1(raw, tile):
+            nc.scalar.copy(
+                tile.rearrange("p (u e m j) -> p u m j e", u=2, e=2, j=4),
+                raw.rearrange("p j (m u e) -> p u m j e", u=2, e=2),
+            )
+            return tile
+
+        def quantise(codes, scales, src):
+            nc.vector.quantize_mx(codes.bitcast(FP8X4), scales, src)
+
+        def gather_table(a, lo, hi):
+            nc.vector.tensor_copy(
+                v_codes[a][:, lo:hi], tabs[a][:].bitcast(U32).indirect(idx1[:, lo // 16:hi // 16])
+            )
+
+        gather_table(0, 0, S)
+        nc.vector.tensor_copy(v_sc[:], tab_sc[:].indirect(idx1[:]))
+        for a in range(PASS1):
+            rounded = round_w1(raw0[a][:], staging("w0r%d" % a)[:])
+            quantise(w_codes[0][a], w_sc[0][a][:], rounded)
+        gather_table(1, 0, S)
+        gather_table(2, 0, BANK)
+        gather_table(2, BANK, S)
+        raw1 = sb([P, PASS1, 4, KP], F32, "raw1", tag="close")
+        for a in range(PASS1):
+            load_w1(raw1[:, a, :, :], a, 1)
+
+        def distances(b, t):
+            step = 4 * b + t
+            tag, bufs = (("big1", "w_codes1", "big2")[step], 1) if step < 3 else ("h", 3)
+            h = sb([P, S], F32, "h%d" % step, tag=tag, bufs=bufs)
+            for lo in range(0, S, BANK):
+                acc = psum.tile([P, BANK], F32, name="acc1", tag="acc1")
+                for a in range(PASS1):
+                    nc.tensor.matmul_mx(
+                        acc[:],
+                        lhsT=w_codes[b][a][:, t * P:(t + 1) * P].bitcast(FP8X4),
+                        lhsT_scale=w_sc[b][a][:, t * P:(t + 1) * P],
+                        rhs=v_codes[a][:, lo:lo + BANK].bitcast(FP8X4),
+                        rhs_scale=v_sc[4 * a:P, lo:lo + BANK],
+                        start=(a == 0), stop=(a == PASS1 - 1),
+                    )
+                nc.scalar.activation(h[:, lo:lo + BANK], acc[:], ACT.Square, bias=cen[:, b, t:t + 1], scale=-1.0)
+            return h
+
+        def place(h, t, page, lo, hi):
+            nc.vector.tensor_tensor(
+                page[:].indirect(idx2[:, lo // 16:hi // 16]), h[:, lo:hi], wgs_sb[t][:, lo:hi], MULT
+            )
+
+        hs = [distances(0, 0)]
+        place(hs[0], 0, pages[0], 0, BANK)
+        place(hs[0], 0, pages[0], BANK, S)
+        hs.append(distances(0, 1))
+
+        place(hs[1], 1, pages[1], 0, S)
+        hs.append(distances(0, 2))
+        rounded1 = sb([P, PASS1, 4 * KP], BF16, "rounded1", tag="big0")
+        codes1 = sb([P, PASS1, KP], U32, "w_codes1")
+        w_codes.append([codes1[:, a, :] for a in range(PASS1)])
+        for a in range(PASS1):
+            round_w1(raw1[:, a, :, :], rounded1[:, a, :])
+            quantise(w_codes[1][a], w_sc[1][a][:], rounded1[:, a, :])
+
+        beds = {(0, 0): load_bed(0, 0, 0), (0, 1): load_bed(0, 1, 1)}
+        w4_sb = sb([P, PASS2, 2 * N], U8, "w4_sb")
+        nc.sync.dma_start(w4_sb[:].bitcast(I32), w4_words.bitcast(I32).rearrange("a p w -> p a w"))
+        for q in QUADS:
+            nc.sync.dma_start(
+                w4_sc[32 * q:32 * q + 4, :, :].bitcast(I32),
+                w4_scales[:, 4 * q:4 * q + 4, :].bitcast(I32).rearrange("a r c -> r a c"),
+            )
+        idx3 = load_list(offs3, "idx3")
+        idx4 = load_list(offs4, "idx4")
+
+        close = sb([P, 4 * T2], F32, "close", tag="close")
+        z_codes = [sb([P, T2], U32, "z_codes%d" % b) for b in range(PASS2)]
+        z_sc = [sb([P, T2], U8, "z_sc%d" % b) for b in range(PASS2)]
+
+        def close_chunk(lo, width):
+            return close[:, 4 * lo:4 * (lo + width)].rearrange("p (t c) -> p t c", t=4)
+
+        def closeness(page, t, chunks):
+            for lo, width in chunks:
+                nc.scalar.activation(close_chunk(lo, width)[:, t, :], page[:, lo:lo + width], ACT.Exp, scale=-1.0)
+
+        def weigh(b, lo, width):
+            tile = staging("z%d_%d" % (b, lo))
+            half, at = divmod(lo, T2 // 2)
+            nc.vector.tensor_tensor(
+                tile[:, 0:4 * width].rearrange("p (c i t) -> p c t i", i=2, t=4),
+                close_chunk(lo, width).rearrange("p t (c i) -> p c t i", i=2),
+                beds[(b, half)][:, :, at:at + width].rearrange("p t (c i) -> p c t i", i=2),
+                MULT,
+            )
+            return tile
+
+        ys = []
+
+        def features(lo, width):
+            step = BANK if width == BANK else P
+            for n in range(NT):
+                acc = psum.tile([P, BANK], F32, name="acc2", tag="acc2")
+                for at in range(0, width, step):
+                    cols = slice(lo + at, lo + at + step)
+                    for b in range(PASS2):
+                        nc.tensor.matmul_mx(
+                            acc[:, at:at + step],
+                            lhsT=w4_sb[:, b, 2 * n * P:2 * (n + 1) * P].bitcast(FP4X4),
+                            lhsT_scale=w4_sc[:, b, n * P:(n + 1) * P],
+                            rhs=z_codes[b][:, cols].bitcast(FP8X4),
+                            rhs_scale=z_sc[b][:, cols],
+                            start=(b == 0), stop=(b == PASS2 - 1),
+                        )
+                nc.scalar.copy(ys[n][:, lo:lo + width], acc[:, 0:width])
+
+        def make_z(b, chunks):
+            waiting = None
+            for chunk in chunks + [None]:
+                made = (chunk, weigh(b, *chunk)) if chunk else None
+                if waiting:
+                    (lo, width), tile = waiting
+                    quantise(z_codes[b][:, lo:lo + width], z_sc[b][:, lo:lo + width], tile[:, 0:4 * width])
+                    if b == PASS2 - 1:
+                        features(lo, width)
+                waiting = made
+
+        for step in range(4 * PASS2):
+            b, t = divmod(step, 4)
+            page = pages[step % PAGES]
+            if step > 1:
+                place(hs[step], t, page, 0, S)
+            if step == 2:
+                beds[(1, 0)] = load_bed(1, 0, 2)
+            if 2 < step + 2 < 4 * PASS2:
+                hs.append(distances(*divmod(step + 2, 4)))
+            if step == 4:
+                make_z(0, CHUNKS0)
+                beds[(1, 1)] = load_bed(1, 1, 0)
+                wgo_sb = sb([P, PK], F32, "wgo_sb", tag="wgs0")
+                nc.sync.dma_start(wgo_sb[:], wgo)
+            closeness(page, t, CHUNKS0 if b == 0 else CHUNKS1)
+        ys.extend([sb([P, T2], F32, "y%d" % n, tag="y%d" % n) for n in range(NT)])
+        make_z(1, CHUNKS1)
+
+        picked = []
+        for n in range(NT):
+            x = sb([P, PK], F32, "x%d" % n, tag="h", bufs=3)
+            width = PK // 2 if n == 0 else PK
+            for lo in range(0, PK, width):
+                part = x[:, lo:lo + width]
+                nc.vector.tensor_copy(part, ys[n][:].indirect(idx3[:, lo // 16:(lo + width) // 16]))
+                nc.scalar.activation(part, part, ACT.Square)
+                nc.scalar.activation(part, part, ACT.Ln, bias=1.0)
+            picked.append(x)
+        for n in range(NT):
+            desk = outs[n % OUTS]
+            nc.vector.tensor_tensor(desk[:].indirect(idx4[:]), picked[n][:], wgo_sb[:], MULT)
+            nc.sync.dma_start(out[n * P:(n + 1) * P, :], desk[:])

@@ -24,9 +24,19 @@ NT = N // P
 BANK = 512
 PAGES = 3
 OUTS = 2
+KIB = 1024
 QUADS = (0, 2, 1, 3)
+SCALE_ROW0 = (0, 16, 80)
 CHUNKS0 = [(0, 512), (512, 512), (1024, 512), (1536, 512)]
 CHUNKS1 = [(0, 128), (128, 128), (256, 256), (512, 512), (1024, 512), (1536, 256), (1792, 128), (1920, 128)]
+
+AT_PAGE, AT_VCODES, AT_WCODES, AT_Y = 0, 24, 36, 24
+AT_PICKED_SC, AT_WSC, AT_W4, AT_W4SC, AT_CEN = 49, 50, 53, 54.5, 55.5
+AT_VSC = 92
+AT_ZCODES, AT_ZSC, AT_WGS, AT_WGO, AT_H, AT_STAGE = 56, 72, 76, 232, 96, 108
+AT_TAB, AT_RAW0, AT_TABSC = (120, 136, 152), (168, 184, 192), 232
+AT_H_FIRST = (168, 120, 200)
+AT_RAW1, AT_CLOSE, AT_BED, AT_DESK = 152, 152, (120, 200), 184
 
 
 def tile_list_bed_request_matching_kernel(
@@ -39,8 +49,8 @@ def tile_list_bed_request_matching_kernel(
         keep = ctx.enter_context(tc.tile_pool(name="keep", bufs=1))
         psum = ctx.enter_context(tc.psum_pool(name="psum", bufs=4))
 
-        def sb(shape, dtype, name, tag=None, bufs=1):
-            return keep.tile(shape, dtype, name=name, tag=tag or name, bufs=bufs, align_bytes=64)
+        def sb(shape, dtype, name, at):
+            return keep.tile(shape, dtype, name=name, tag=name, align_bytes=64, offset=int(at * KIB))
 
         def load_list(src, name):
             tile = lists.tile([P, S // 16], U16, name=name)
@@ -48,7 +58,7 @@ def tile_list_bed_request_matching_kernel(
             return tile
 
         def load_table(a):
-            tile = sb([P, T], I32, "tab%d" % a, tag=("big0", "big1", "close")[a])
+            tile = sb([P, T], I32, "tab%d" % a, AT_TAB[a])
             nc.sync.dma_start(tile[:], tab_words[a].rearrange("p t i -> p (t i)").bitcast(I32))
             return tile
 
@@ -57,56 +67,60 @@ def tile_list_bed_request_matching_kernel(
             nc.sync.dma_start(dst, rows.rearrange("(p j) c -> p j c", j=4))
 
         def load_wgs(t0, t1):
-            tile = sb([P, t1 - t0, S], F32, "wgs%d" % t0)
+            tile = sb([P, t1 - t0, S], F32, "wgs%d" % t0, AT_WGS + 4 * t0)
             src = wgs.rearrange("(q t) j -> q t j", t=4)[:, t0:t1, :]
             for q in QUADS:
                 nc.sync.dma_start(tile[32 * q:32 * q + 32, :, :], src)
             return [tile[:, i, :] for i in range(t1 - t0)]
 
-        def load_bed(b, half, slot):
-            tile = sb([P, 4, T2 // 2], F32, "bed%d%d" % (b, half), tag="big%d" % slot)
-            cols = slice(half * (T2 // 2), (half + 1) * (T2 // 2))
-            nc.sync.dma_start(tile[:], bedw[b * KP:(b + 1) * KP, cols].rearrange("(p t) c -> p t c", t=4))
+        def load_bed(b):
+            tile = sb([P, 4, T2], F32, "bed%d" % b, AT_BED[b])
+            nc.sync.dma_start(tile[:], bedw[b * KP:(b + 1) * KP, :].rearrange("(p t) c -> p t c", t=4))
             return tile
 
-        def staging(name):
-            return sb([P, 4 * KP], BF16, name, tag="stage", bufs=3)
+        staged = []
 
-        tab_sc = sb([P, T], U8, "tab_sc", tag="h", bufs=3)
-        nc.vector.memset(tab_sc[:].bitcast(I32), 0)
-        for q in QUADS:
-            nc.gpsimd.dma_start(
-                tab_sc[32 * q:32 * q + 4 * PASS1, :].bitcast(I32),
-                tab_scales[:, 4 * q:4 * q + 4, :].bitcast(I32),
-            )
-        w4_sc = sb([P, PASS2, N], U8, "w4_sc")
-        nc.vector.memset(w4_sc[:].rearrange("p a c -> p (a c)").bitcast(I32), 0)
-        pages = [sb([P, T2], F32, "page%d" % i) for i in range(PAGES)]
-        outs = [sb([P, T2], F32, "desk%d" % i) for i in range(OUTS)]
-        for tile in pages + outs:
-            nc.vector.memset(tile[:], 0.0)
+        def staging():
+            staged.append(sb([P, 4 * KP], BF16, "stage%d" % len(staged), AT_STAGE + 4 * (len(staged) % 3)))
+            return staged[-1]
 
         idx1 = load_list(offs, "idx1")
-        idx2 = load_list(offs2, "idx2")
-        cen = sb([P, PASS2, 4], F32, "cen")
-        nc.sync.dma_start(cen[:], centre.rearrange("(b p t) -> p b t", b=PASS2, t=4))
-        raw0 = [sb([P, 4, KP], F32, "raw0_%d" % a, tag="y%d" % a) for a in range(PASS1)]
+        tab_sc = sb([P, T], U8, "tab_sc", AT_TABSC)
+        scale_rows = tab_scales.rearrange("a q t -> (a q) t").bitcast(I32)
+        nc.sync.dma_start(tab_sc[0:32, :].bitcast(I32), scale_rows[0:32])
+        nc.sync.dma_start(tab_sc[64:96, :].bitcast(I32), scale_rows[16:48])
+        for q in (1, 3):
+            nc.vector.memset(tab_sc[32 * q:32 * q + 32, :].bitcast(I32), 0)
+        v_sc = sb([P, PASS1 * S], U8, "v_sc", AT_VSC)
+        nc.vector.memset(v_sc[:].bitcast(I32), 0)
+        w4_sc = sb([P, PASS2, N], U8, "w4_sc", AT_W4SC)
+        nc.vector.memset(w4_sc[:].rearrange("p a c -> p (a c)").bitcast(I32), 0)
+        pages = [sb([P, T2], F32, "page%d" % i, AT_PAGE + 8 * i) for i in range(PAGES)]
+        nc.vector.memset(pages[0][:], 0.0)
+
+        cen = sb([P, PASS2, 4], F32, "cen", AT_CEN)
+        nc.gpsimd.dma_start(cen[:], centre.rearrange("(b p t) -> p b t", b=PASS2, t=4))
+        raw0 = [sb([P, 4, KP], F32, "raw0_%d" % a, AT_RAW0[a]) for a in range(PASS1)]
         tabs = [load_table(0)]
-        for a in range(PASS1):
-            load_w1(raw0[a][:], a, 0)
-        tabs.extend([load_table(a) for a in range(1, PASS1)])
+        load_w1(raw0[0][:], 0, 0)
+        load_w1(raw0[1][:], 1, 0)
+        tabs.append(load_table(1))
+        load_w1(raw0[2][:], 2, 0)
+        tabs.append(load_table(2))
+        idx2 = load_list(offs2, "idx2")
         wgs_sb = load_wgs(0, 1)
-        wgs_sb.extend(load_wgs(1, 2))
-        wgs_sb.extend(load_wgs(2, 4))
+        wgs_sb.extend(load_wgs(1, 4))
 
-        v_codes = [sb([P, S], U32, "v_codes%d" % a) for a in range(PASS1)]
-        v_sc = sb([P, S], U8, "v_sc")
-        w_codes = [[sb([P, KP], U32, "w_codes0%d" % a)[:] for a in range(PASS1)]]
-        w_sc = [[sb([P, KP], U8, "w_sc%d%d" % (b, a)) for a in range(PASS1)] for b in range(PASS2)]
+        v_codes = [sb([P, S], U32, "v_codes%d" % a, AT_VCODES + 4 * a) for a in range(PASS1)]
+        w_codes = [[sb([P, KP], U32, "w_codes%d%d" % (b, a), AT_WCODES + 6 * b + 2 * a) for a in range(PASS1)]
+                   for b in range(PASS2)]
+        w_sc = [[sb([P, KP], U8, "w_sc%d%d" % (b, a), AT_WSC + 1.5 * b + 0.5 * a) for a in range(PASS1)]
+                for b in range(PASS2)]
 
-        def round_w1(raw, tile):
+        def round_w1(raw):
+            tile = staging()
             nc.scalar.copy(
-                tile.rearrange("p (u e m j) -> p u m j e", u=2, e=2, j=4),
+                tile[:].rearrange("p (u e m j) -> p u m j e", u=2, e=2, j=4),
                 raw.rearrange("p j (m u e) -> p u m j e", u=2, e=2),
             )
             return tile
@@ -119,23 +133,33 @@ def tile_list_bed_request_matching_kernel(
                 v_codes[a][:, lo:hi], tabs[a][:].bitcast(U32).indirect(idx1[:, lo // 16:hi // 16])
             )
 
-        gather_table(0, 0, S)
-        nc.vector.tensor_copy(v_sc[:], tab_sc[:].indirect(idx1[:]))
+        picked_sc = sb([P, S], U8, "picked_sc", AT_PICKED_SC)
+        nc.vector.tensor_copy(picked_sc[:], tab_sc[:].indirect(idx1[:]))
         for a in range(PASS1):
-            rounded = round_w1(raw0[a][:], staging("w0r%d" % a)[:])
-            quantise(w_codes[0][a], w_sc[0][a][:], rounded)
+            for q in QUADS:
+                row = SCALE_ROW0[a] + 4 * q
+                nc.gpsimd.dma_start(
+                    v_sc[32 * q:32 * q + 4, a * S:(a + 1) * S].bitcast(I32), picked_sc[row:row + 4, :].bitcast(I32)
+                )
+        gather_table(0, 0, S)
+        for tile in pages[1:]:
+            nc.vector.memset(tile[:], 0.0)
+        for a in range(2):
+            quantise(w_codes[0][a][:], w_sc[0][a][:], round_w1(raw0[a][:])[:])
         gather_table(1, 0, S)
+        quantise(w_codes[0][2][:], w_sc[0][2][:], round_w1(raw0[2][:])[:])
         gather_table(2, 0, BANK)
         gather_table(2, BANK, S)
-        raw1 = sb([P, PASS1, 4, KP], F32, "raw1", tag="close")
-        for a in range(PASS1):
-            load_w1(raw1[:, a, :, :], a, 1)
+        outs = [sb([P, T2], F32, "desk%d" % i, AT_DESK + 8 * i) for i in range(OUTS)]
+        for tile in outs:
+            nc.gpsimd.memset(tile[:], 0.0)
 
-        def distances(b, t):
-            step = 4 * b + t
-            tag, bufs = (("big1", "w_codes1", "big2")[step], 1) if step < 3 else ("h", 3)
-            h = sb([P, S], F32, "h%d" % step, tag=tag, bufs=bufs)
+        def distances(step):
+            b, t = divmod(step, 4)
+            at = AT_H_FIRST[step] if step < 3 else AT_H + 4 * (step % 3)
+            h = [sb([P, BANK], F32, "h%d_%d" % (step, i), at + 8 * i) for i in range(2)] if step == 0 else sb([P, S], F32, "h%d" % step, at)
             for lo in range(0, S, BANK):
+                dst = h[lo // BANK][:] if step == 0 else h[:, lo:lo + BANK]
                 acc = psum.tile([P, BANK], F32, name="acc1", tag="acc1")
                 for a in range(PASS1):
                     nc.tensor.matmul_mx(
@@ -143,33 +167,24 @@ def tile_list_bed_request_matching_kernel(
                         lhsT=w_codes[b][a][:, t * P:(t + 1) * P].bitcast(FP8X4),
                         lhsT_scale=w_sc[b][a][:, t * P:(t + 1) * P],
                         rhs=v_codes[a][:, lo:lo + BANK].bitcast(FP8X4),
-                        rhs_scale=v_sc[4 * a:P, lo:lo + BANK],
+                        rhs_scale=v_sc[:, a * S + lo:a * S + lo + BANK],
                         start=(a == 0), stop=(a == PASS1 - 1),
                     )
-                nc.scalar.activation(h[:, lo:lo + BANK], acc[:], ACT.Square, bias=cen[:, b, t:t + 1], scale=-1.0)
+                nc.scalar.activation(dst, acc[:], ACT.Square, bias=cen[:, b, t:t + 1], scale=-1.0)
             return h
 
         def place(h, t, page, lo, hi):
             nc.vector.tensor_tensor(
-                page[:].indirect(idx2[:, lo // 16:hi // 16]), h[:, lo:hi], wgs_sb[t][:, lo:hi], MULT
+                page[:].indirect(idx2[:, lo // 16:hi // 16]), h, wgs_sb[t][:, lo:hi], MULT
             )
 
-        hs = [distances(0, 0)]
-        place(hs[0], 0, pages[0], 0, BANK)
-        place(hs[0], 0, pages[0], BANK, S)
-        hs.append(distances(0, 1))
+        hs = [distances(step) for step in range(4)]
+        place(hs[0][0][:], 0, pages[0], 0, BANK)
+        place(hs[0][1][:], 0, pages[0], BANK, S)
+        place(hs[1][:], 1, pages[1], 0, S)
+        place(hs[2][:], 2, pages[2], 0, S)
 
-        place(hs[1], 1, pages[1], 0, S)
-        hs.append(distances(0, 2))
-        rounded1 = sb([P, PASS1, 4 * KP], BF16, "rounded1", tag="big0")
-        codes1 = sb([P, PASS1, KP], U32, "w_codes1")
-        w_codes.append([codes1[:, a, :] for a in range(PASS1)])
-        for a in range(PASS1):
-            round_w1(raw1[:, a, :, :], rounded1[:, a, :])
-            quantise(w_codes[1][a], w_sc[1][a][:], rounded1[:, a, :])
-
-        beds = {(0, 0): load_bed(0, 0, 0), (0, 1): load_bed(0, 1, 1)}
-        w4_sb = sb([P, PASS2, 2 * N], U8, "w4_sb")
+        w4_sb = sb([P, PASS2, 2 * N], U8, "w4_sb", AT_W4)
         nc.sync.dma_start(w4_sb[:].bitcast(I32), w4_words.bitcast(I32).rearrange("a p w -> p a w"))
         for q in QUADS:
             nc.sync.dma_start(
@@ -178,25 +193,35 @@ def tile_list_bed_request_matching_kernel(
             )
         idx3 = load_list(offs3, "idx3")
         idx4 = load_list(offs4, "idx4")
+        wgo_sb = sb([P, PK], F32, "wgo_sb", AT_WGO)
+        nc.sync.dma_start(wgo_sb[:], wgo)
 
-        close = sb([P, 4 * T2], F32, "close", tag="close")
-        z_codes = [sb([P, T2], U32, "z_codes%d" % b) for b in range(PASS2)]
-        z_sc = [sb([P, T2], U8, "z_sc%d" % b) for b in range(PASS2)]
+        raw1 = sb([P, PASS1, 4, KP], F32, "raw1", AT_RAW1)
+        for a in range(PASS1):
+            load_w1(raw1[:, a, :, :], a, 1)
+        for a in range(PASS1):
+            quantise(w_codes[1][a][:], w_sc[1][a][:], round_w1(raw1[:, a, :, :])[:])
+        beds = [load_bed(b) for b in range(PASS2)]
+
+        close = sb([P, 4 * T2], F32, "close", AT_CLOSE)
+        z_codes = [sb([P, T2], U32, "z_codes%d" % b, AT_ZCODES + 8 * b) for b in range(PASS2)]
+        z_sc = [sb([P, T2], U8, "z_sc%d" % b, AT_ZSC + 2 * b) for b in range(PASS2)]
 
         def close_chunk(lo, width):
             return close[:, 4 * lo:4 * (lo + width)].rearrange("p (t c) -> p t c", t=4)
 
-        def closeness(page, t, chunks):
-            for lo, width in chunks:
+        def closeness(step):
+            b, t = divmod(step, 4)
+            page = pages[step % PAGES]
+            for lo, width in CHUNKS0 if b == 0 else CHUNKS1:
                 nc.scalar.activation(close_chunk(lo, width)[:, t, :], page[:, lo:lo + width], ACT.Exp, scale=-1.0)
 
         def weigh(b, lo, width):
-            tile = staging("z%d_%d" % (b, lo))
-            half, at = divmod(lo, T2 // 2)
+            tile = staging()
             nc.vector.tensor_tensor(
                 tile[:, 0:4 * width].rearrange("p (c i t) -> p c t i", i=2, t=4),
                 close_chunk(lo, width).rearrange("p t (c i) -> p c t i", i=2),
-                beds[(b, half)][:, :, at:at + width].rearrange("p t (c i) -> p c t i", i=2),
+                beds[b][:, :, lo:lo + width].rearrange("p t (c i) -> p c t i", i=2),
                 MULT,
             )
             return tile
@@ -231,27 +256,24 @@ def tile_list_bed_request_matching_kernel(
                         features(lo, width)
                 waiting = made
 
-        for step in range(4 * PASS2):
-            b, t = divmod(step, 4)
-            page = pages[step % PAGES]
-            if step > 1:
-                place(hs[step], t, page, 0, S)
-            if step == 2:
-                beds[(1, 0)] = load_bed(1, 0, 2)
-            if 2 < step + 2 < 4 * PASS2:
-                hs.append(distances(*divmod(step + 2, 4)))
+        closeness(0)
+        hs.append(distances(4))
+        for step in range(3, 4 * PASS2):
+            place(hs[step][:], step % 4, pages[step % PAGES], 0, S)
+            if step + 2 < 4 * PASS2:
+                hs.append(distances(step + 2))
+            if step == 3:
+                closeness(1)
+                closeness(2)
             if step == 4:
                 make_z(0, CHUNKS0)
-                beds[(1, 1)] = load_bed(1, 1, 0)
-                wgo_sb = sb([P, PK], F32, "wgo_sb", tag="wgs0")
-                nc.sync.dma_start(wgo_sb[:], wgo)
-            closeness(page, t, CHUNKS0 if b == 0 else CHUNKS1)
-        ys.extend([sb([P, T2], F32, "y%d" % n, tag="y%d" % n) for n in range(NT)])
+            closeness(step)
+        ys.extend([sb([P, T2], F32, "y%d" % n, AT_Y + 8 * n) for n in range(NT)])
         make_z(1, CHUNKS1)
 
         picked = []
         for n in range(NT):
-            x = sb([P, PK], F32, "x%d" % n, tag="h", bufs=3)
+            x = sb([P, PK], F32, "x%d" % n, AT_H + 4 * n)
             width = PK // 2 if n == 0 else PK
             for lo in range(0, PK, width):
                 part = x[:, lo:lo + width]

@@ -28,15 +28,19 @@ KIB = 1024
 QUADS = (0, 2, 1, 3)
 SCALE_ROW0 = (0, 16, 80)
 CHUNKS0 = [(0, 512), (512, 512), (1024, 512), (1536, 512)]
-CHUNKS1 = [(0, 128), (128, 128), (256, 256), (512, 512), (1024, 512), (1536, 256), (1792, 128), (1920, 128)]
+CHUNKS1 = [(0, 512), (512, 512), (1024, 512), (1536, 256), (1792, 128), (1920, 128)]
 
-AT_PAGE, AT_VCODES, AT_WCODES, AT_Y = 0, 24, 36, 24
-AT_PICKED_SC, AT_WSC, AT_W4, AT_W4SC, AT_CEN = 49, 50, 53, 54.5, 55.5
-AT_VSC = 92
-AT_ZCODES, AT_ZSC, AT_WGS, AT_WGO, AT_H, AT_STAGE = 56, 72, 76, 232, 96, 108
-AT_TAB, AT_RAW0, AT_TABSC = (120, 136, 152), (168, 184, 192), 232
-AT_H_FIRST = (168, 120, 200)
-AT_RAW1, AT_CLOSE, AT_BED, AT_DESK = 152, 152, (120, 200), 184
+AT_PAGE, AT_VCODES, AT_WCODES, AT_Y = 0, 24, (179, 36), 24
+AT_PICKED_SC, AT_WSC, AT_CEN = 49, 50, 55.5
+AT_X, AT_ZCODES, AT_ZSC, AT_VSC = (84, 56, 60), (128, 64), 72, 80
+AT_WGS, AT_WGO = (76, 96, 100), 76
+AT_W4, AT_W4SC, AT_STAGE, AT_DESK = 140, 141.5, 143, 145
+AT_TAB, AT_RAW0, AT_TABSC = (108, 124, 155), (171, 187, 195), 203
+AT_H = 84
+AT_HS = (114, 126, 132, 203, 108, 116, 124, 128)
+BED0_PIECES = ((0, 0, 1024), (0, 1024, 1024), (1, 0, 512), (1, 512, 512), (1, 1024, 1024))
+AT_RAW1, AT_CLOSE, AT_BED0, AT_BED1, AT_Z0 = 155, 155, 108, 203, 187
+PAIR_COLS = 256
 
 
 def tile_list_bed_request_matching_kernel(
@@ -67,22 +71,20 @@ def tile_list_bed_request_matching_kernel(
             nc.sync.dma_start(dst, rows.rearrange("(p j) c -> p j c", j=4))
 
         def load_wgs(t0, t1):
-            tile = sb([P, t1 - t0, S], F32, "wgs%d" % t0, AT_WGS + 4 * t0)
+            tile = sb([P, t1 - t0, S], F32, "wgs%d" % t0, AT_WGS[t0])
             src = wgs.rearrange("(q t) j -> q t j", t=4)[:, t0:t1, :]
             for q in QUADS:
                 nc.sync.dma_start(tile[32 * q:32 * q + 32, :, :], src)
             return [tile[:, i, :] for i in range(t1 - t0)]
 
-        def load_bed(b):
-            tile = sb([P, 4, T2], F32, "bed%d" % b, AT_BED[b])
-            nc.sync.dma_start(tile[:], bedw[b * KP:(b + 1) * KP, :].rearrange("(p t) c -> p t c", t=4))
+        def load_bed(b, t0, t1, lo, width, at):
+            tile = sb([P, t1 - t0, width], F32, "bed%d%d_%d" % (b, t0, lo), at)
+            rows = bedw[b * KP:(b + 1) * KP, lo:lo + width].rearrange("(p t) c -> p t c", t=4)
+            nc.sync.dma_start(tile[:], rows[:, t0:t1, :])
             return tile
 
-        staged = []
-
-        def staging():
-            staged.append(sb([P, 4 * KP], BF16, "stage%d" % len(staged), AT_STAGE + 4 * (len(staged) % 3)))
-            return staged[-1]
+        def staging(name, slot, slots=1):
+            return sb([P, slots * 4 * KP], BF16, name, AT_STAGE + 4 * slot)
 
         idx1 = load_list(offs, "idx1")
         tab_sc = sb([P, T], U8, "tab_sc", AT_TABSC)
@@ -93,11 +95,7 @@ def tile_list_bed_request_matching_kernel(
             nc.vector.memset(tab_sc[32 * q:32 * q + 32, :].bitcast(I32), 0)
         v_sc = sb([P, PASS1 * S], U8, "v_sc", AT_VSC)
         nc.vector.memset(v_sc[:].bitcast(I32), 0)
-        w4_sc = sb([P, PASS2, N], U8, "w4_sc", AT_W4SC)
-        nc.vector.memset(w4_sc[:].rearrange("p a c -> p (a c)").bitcast(I32), 0)
         pages = [sb([P, T2], F32, "page%d" % i, AT_PAGE + 8 * i) for i in range(PAGES)]
-        nc.vector.memset(pages[0][:], 0.0)
-
         cen = sb([P, PASS2, 4], F32, "cen", AT_CEN)
         nc.gpsimd.dma_start(cen[:], centre.rearrange("(b p t) -> p b t", b=PASS2, t=4))
         raw0 = [sb([P, 4, KP], F32, "raw0_%d" % a, AT_RAW0[a]) for a in range(PASS1)]
@@ -107,26 +105,23 @@ def tile_list_bed_request_matching_kernel(
         tabs.append(load_table(1))
         load_w1(raw0[2][:], 2, 0)
         tabs.append(load_table(2))
-        idx2 = load_list(offs2, "idx2")
-        wgs_sb = load_wgs(0, 1)
-        wgs_sb.extend(load_wgs(1, 4))
 
         v_codes = [sb([P, S], U32, "v_codes%d" % a, AT_VCODES + 4 * a) for a in range(PASS1)]
-        w_codes = [[sb([P, KP], U32, "w_codes%d%d" % (b, a), AT_WCODES + 6 * b + 2 * a) for a in range(PASS1)]
-                   for b in range(PASS2)]
-        w_sc = [[sb([P, KP], U8, "w_sc%d%d" % (b, a), AT_WSC + 1.5 * b + 0.5 * a) for a in range(PASS1)]
-                for b in range(PASS2)]
+        w_codes = [sb([P, PASS1 * KP], U32, "w_codes%d" % b, AT_WCODES[b]) for b in range(PASS2)]
+        w_sc = [sb([P, PASS1 * KP], U8, "w_sc%d" % b, AT_WSC + 1.5 * b) for b in range(PASS2)]
 
-        def round_w1(raw):
-            tile = staging()
+        def round_w1(dst, raw):
             nc.scalar.copy(
-                tile[:].rearrange("p (u e m j) -> p u m j e", u=2, e=2, j=4),
+                dst.rearrange("p (u e m j) -> p u m j e", u=2, e=2, j=4),
                 raw.rearrange("p j (m u e) -> p u m j e", u=2, e=2),
             )
-            return tile
 
         def quantise(codes, scales, src):
             nc.vector.quantize_mx(codes.bitcast(FP8X4), scales, src)
+
+        def quantise_w1(b, a0, a1, src):
+            cols = slice(a0 * KP, a1 * KP)
+            quantise(w_codes[b][:, cols], w_sc[b][:, cols], src)
 
         def gather_table(a, lo, hi):
             nc.vector.tensor_copy(
@@ -136,54 +131,77 @@ def tile_list_bed_request_matching_kernel(
         picked_sc = sb([P, S], U8, "picked_sc", AT_PICKED_SC)
         nc.vector.tensor_copy(picked_sc[:], tab_sc[:].indirect(idx1[:]))
         for a in range(PASS1):
-            for q in QUADS:
-                row = SCALE_ROW0[a] + 4 * q
-                nc.gpsimd.dma_start(
-                    v_sc[32 * q:32 * q + 4, a * S:(a + 1) * S].bitcast(I32), picked_sc[row:row + 4, :].bitcast(I32)
+            for r in range(4):
+                row = SCALE_ROW0[a] + r
+                (nc.sync if a == PASS1 - 1 else nc.gpsimd).dma_start(
+                    v_sc[r:P:32, a * S:(a + 1) * S].bitcast(I32), picked_sc[row:row + 13:4, :].bitcast(I32)
                 )
+        wgs_sb = load_wgs(0, 1)
+        idx2 = load_list(offs2, "idx2")
+        wgs_sb.extend(load_wgs(1, 2))
+
+        nc.vector.memset(pages[0][:], 0.0)
         gather_table(0, 0, S)
         for tile in pages[1:]:
             nc.vector.memset(tile[:], 0.0)
-        for a in range(2):
-            quantise(w_codes[0][a][:], w_sc[0][a][:], round_w1(raw0[a][:])[:])
-        gather_table(1, 0, S)
-        quantise(w_codes[0][2][:], w_sc[0][2][:], round_w1(raw0[2][:])[:])
+        w4_sc = sb([P, PASS2, N], U8, "w4_sc", AT_W4SC)
+        nc.vector.memset(w4_sc[:].rearrange("p a c -> p (a c)").bitcast(I32), 0)
+        for a in range(PASS1):
+            if a == PASS1 - 1:
+                gather_table(1, 0, S)
+            rounded = staging("w0r%d" % a, a)
+            round_w1(rounded[:], raw0[a][:])
+            quantise_w1(0, a, a + 1, rounded[:])
         gather_table(2, 0, BANK)
         gather_table(2, BANK, S)
-        outs = [sb([P, T2], F32, "desk%d" % i, AT_DESK + 8 * i) for i in range(OUTS)]
-        for tile in outs:
-            nc.gpsimd.memset(tile[:], 0.0)
+
+        raw1 = sb([P, PASS1, 4, KP], F32, "raw1", AT_RAW1)
+        for a in range(PASS1):
+            load_w1(raw1[:, a, :, :], a, 1)
+        wgs_sb.extend(load_wgs(2, 4))
 
         def distances(step):
             b, t = divmod(step, 4)
-            at = AT_H_FIRST[step] if step < 3 else AT_H + 4 * (step % 3)
-            h = [sb([P, BANK], F32, "h%d_%d" % (step, i), at + 8 * i) for i in range(2)] if step == 0 else sb([P, S], F32, "h%d" % step, at)
+            h = sb([P, S], F32, "h%d" % step, AT_H + 4 * (step % 3))
+            placed = sb([P, S], F32, "placed%d" % step, AT_HS[step])
             for lo in range(0, S, BANK):
-                dst = h[lo // BANK][:] if step == 0 else h[:, lo:lo + BANK]
                 acc = psum.tile([P, BANK], F32, name="acc1", tag="acc1")
                 for a in range(PASS1):
+                    cols = slice(a * KP + t * P, a * KP + (t + 1) * P)
                     nc.tensor.matmul_mx(
                         acc[:],
-                        lhsT=w_codes[b][a][:, t * P:(t + 1) * P].bitcast(FP8X4),
-                        lhsT_scale=w_sc[b][a][:, t * P:(t + 1) * P],
+                        lhsT=w_codes[b][:, cols].bitcast(FP8X4),
+                        lhsT_scale=w_sc[b][:, cols],
                         rhs=v_codes[a][:, lo:lo + BANK].bitcast(FP8X4),
                         rhs_scale=v_sc[:, a * S + lo:a * S + lo + BANK],
                         start=(a == 0), stop=(a == PASS1 - 1),
                     )
-                nc.scalar.activation(dst, acc[:], ACT.Square, bias=cen[:, b, t:t + 1], scale=-1.0)
-            return h
+                part = h[:, lo:lo + BANK]
+                nc.scalar.activation(part, acc[:], ACT.Square, bias=cen[:, b, t:t + 1], scale=-1.0)
+                nc.gpsimd.tensor_tensor(placed[:, lo:lo + BANK], part, wgs_sb[t][:, lo:lo + BANK], MULT)
+            return placed
 
-        def place(h, t, page, lo, hi):
-            nc.vector.tensor_tensor(
-                page[:].indirect(idx2[:, lo // 16:hi // 16]), h, wgs_sb[t][:, lo:hi], MULT
-            )
+        def place(step, lo=0, hi=S):
+            nc.vector.tensor_copy(pages[step % PAGES][:].indirect(idx2[:, lo // 16:hi // 16]), hs[step][:, lo:hi])
 
         hs = [distances(step) for step in range(4)]
-        place(hs[0][0][:], 0, pages[0], 0, BANK)
-        place(hs[0][1][:], 0, pages[0], BANK, S)
-        place(hs[1][:], 1, pages[1], 0, S)
-        place(hs[2][:], 2, pages[2], 0, S)
+        place(0, 0, BANK)
+        place(0, BANK, S)
+        place(1)
 
+        rounded = staging("w1r0", 0)
+        round_w1(rounded[:], raw1[:, 0, :, :])
+        quantise_w1(1, 0, 1, rounded[:])
+        place(2)
+        rounded = staging("w1r12", 1, 2)
+        for a in (1, 2):
+            round_w1(rounded[:, (a - 1) * 4 * KP:a * 4 * KP], raw1[:, a, :, :])
+        quantise_w1(1, 1, 3, rounded[:])
+
+        bed0 = {
+            (pair, lo): load_bed(0, 2 * pair, 2 * pair + 2, lo, width, AT_BED0 + 16 * pair + lo // 128)
+            for pair, lo, width in BED0_PIECES
+        }
         w4_sb = sb([P, PASS2, 2 * N], U8, "w4_sb", AT_W4)
         nc.sync.dma_start(w4_sb[:].bitcast(I32), w4_words.bitcast(I32).rearrange("a p w -> p a w"))
         for q in QUADS:
@@ -193,40 +211,74 @@ def tile_list_bed_request_matching_kernel(
             )
         idx3 = load_list(offs3, "idx3")
         idx4 = load_list(offs4, "idx4")
-        wgo_sb = sb([P, PK], F32, "wgo_sb", AT_WGO)
-        nc.sync.dma_start(wgo_sb[:], wgo)
 
-        raw1 = sb([P, PASS1, 4, KP], F32, "raw1", AT_RAW1)
-        for a in range(PASS1):
-            load_w1(raw1[:, a, :, :], a, 1)
-        for a in range(PASS1):
-            quantise(w_codes[1][a][:], w_sc[1][a][:], round_w1(raw1[:, a, :, :])[:])
-        beds = [load_bed(b) for b in range(PASS2)]
-
-        close = sb([P, 4 * T2], F32, "close", AT_CLOSE)
-        z_codes = [sb([P, T2], U32, "z_codes%d" % b, AT_ZCODES + 8 * b) for b in range(PASS2)]
+        close = sb([P, 4, T2], F32, "close", AT_CLOSE)
+        z0_pairs = sb([P, 2, 2 * T2], BF16, "z0_pairs", AT_Z0)
         z_sc = [sb([P, T2], U8, "z_sc%d" % b, AT_ZSC + 2 * b) for b in range(PASS2)]
 
-        def close_chunk(lo, width):
-            return close[:, 4 * lo:4 * (lo + width)].rearrange("p (t c) -> p t c", t=4)
+        def closeness(step, chunks=CHUNKS0):
+            for lo, width in chunks:
+                nc.scalar.activation(
+                    close[:, step % 4, lo:lo + width], pages[step % PAGES][:, lo:lo + width], ACT.Exp, scale=-1.0
+                )
 
-        def closeness(step):
-            b, t = divmod(step, 4)
-            page = pages[step % PAGES]
-            for lo, width in CHUNKS0 if b == 0 else CHUNKS1:
-                nc.scalar.activation(close_chunk(lo, width)[:, t, :], page[:, lo:lo + width], ACT.Exp, scale=-1.0)
+        def weigh_pair(piece):
+            pair, first, width = BED0_PIECES[piece]
+            rows = slice(2 * pair, 2 * pair + 2)
+            for lo in range(first, first + width, PAIR_COLS):
+                cols = slice(lo, lo + PAIR_COLS)
+                nc.gpsimd.tensor_tensor(
+                    z0_pairs[:, pair, :].rearrange("p (c t) -> p c t", t=2)[:, cols, :],
+                    close[:, rows, cols].rearrange("p t c -> p c t"),
+                    bed0[(pair, first)][:, :, lo - first:lo - first + PAIR_COLS].rearrange("p t c -> p c t"),
+                    MULT,
+                )
 
-        def weigh(b, lo, width):
-            tile = staging()
+        closeness(0)
+        closeness(1)
+        weigh_pair(0)
+        hs.append(distances(4))
+        place(3)
+        bed1 = load_bed(1, 0, 4, 0, T2, AT_BED1)
+        closeness(2)
+        weigh_pair(1)
+        hs.append(distances(5))
+        place(4)
+        wgo_sb = sb([P, PK], F32, "wgo_sb", AT_WGO)
+        nc.sync.dma_start(wgo_sb[:], wgo)
+        closeness(3)
+        weigh_pair(2)
+        hs.append(distances(6))
+        place(5)
+        weigh_pair(3)
+        hs.append(distances(7))
+        closeness(4)
+        weigh_pair(4)
+        z0 = sb([P, 4 * T2], BF16, "z0", AT_VCODES)
+        for lo in range(0, T2, BANK):
+            nc.scalar.copy(
+                z0[:, 4 * lo:4 * (lo + BANK)].bitcast(U32).rearrange("p (c u) -> p c u", u=2),
+                z0_pairs[:].bitcast(U32)[:, :, lo:lo + BANK].rearrange("p u c -> p c u"),
+            )
+        place(6)
+        closeness(5)
+        place(7)
+        closeness(6)
+        closeness(7, CHUNKS1)
+
+        z_codes = [sb([P, T2], U32, "z_codes%d" % b, AT_ZCODES[b]) for b in range(PASS2)]
+        ys = [sb([P, T2], F32, "y%d" % n, AT_Y + 8 * n) for n in range(NT)]
+
+        def weigh(i, lo, width):
+            tile = staging("z1_%d" % i, i % 3)
+            cols = slice(lo, lo + width)
             nc.vector.tensor_tensor(
                 tile[:, 0:4 * width].rearrange("p (c i t) -> p c t i", i=2, t=4),
-                close_chunk(lo, width).rearrange("p t (c i) -> p c t i", i=2),
-                beds[b][:, :, lo:lo + width].rearrange("p t (c i) -> p c t i", i=2),
+                close[:, :, cols].rearrange("p t (c i) -> p c t i", i=2),
+                bed1[:, :, cols].rearrange("p t (c i) -> p c t i", i=2),
                 MULT,
             )
             return tile
-
-        ys = []
 
         def features(lo, width):
             step = BANK if width == BANK else P
@@ -245,35 +297,24 @@ def tile_list_bed_request_matching_kernel(
                         )
                 nc.scalar.copy(ys[n][:, lo:lo + width], acc[:, 0:width])
 
-        def make_z(b, chunks):
-            waiting = None
-            for chunk in chunks + [None]:
-                made = (chunk, weigh(b, *chunk)) if chunk else None
-                if waiting:
-                    (lo, width), tile = waiting
-                    quantise(z_codes[b][:, lo:lo + width], z_sc[b][:, lo:lo + width], tile[:, 0:4 * width])
-                    if b == PASS2 - 1:
-                        features(lo, width)
-                waiting = made
+        for lo in range(0, T2, T2 // 2):
+            cols = slice(lo, lo + T2 // 2)
+            quantise(z_codes[0][:, cols], z_sc[0][:, cols], z0[:, 4 * lo:4 * lo + 2 * T2])
+        waiting = None
+        for i, chunk in enumerate(CHUNKS1 + [None]):
+            made = (chunk, weigh(i, *chunk)) if chunk else None
+            if waiting:
+                (lo, width), tile = waiting
+                quantise(z_codes[1][:, lo:lo + width], z_sc[1][:, lo:lo + width], tile[:, 0:4 * width])
+                features(lo, width)
+            waiting = made
 
-        closeness(0)
-        hs.append(distances(4))
-        for step in range(3, 4 * PASS2):
-            place(hs[step][:], step % 4, pages[step % PAGES], 0, S)
-            if step + 2 < 4 * PASS2:
-                hs.append(distances(step + 2))
-            if step == 3:
-                closeness(1)
-                closeness(2)
-            if step == 4:
-                make_z(0, CHUNKS0)
-            closeness(step)
-        ys.extend([sb([P, T2], F32, "y%d" % n, AT_Y + 8 * n) for n in range(NT)])
-        make_z(1, CHUNKS1)
-
+        outs = [sb([P, T2], F32, "desk%d" % i, AT_DESK + 8 * i) for i in range(OUTS)]
+        for tile in outs:
+            nc.gpsimd.memset(tile[:], 0.0)
         picked = []
         for n in range(NT):
-            x = sb([P, PK], F32, "x%d" % n, AT_H + 4 * n)
+            x = sb([P, PK], F32, "x%d" % n, AT_X[n])
             width = PK // 2 if n == 0 else PK
             for lo in range(0, PK, width):
                 part = x[:, lo:lo + width]

@@ -27,20 +27,21 @@ OUTS = 2
 KIB = 1024
 QUADS = (0, 2, 1, 3)
 SCALE_ROW0 = (0, 16, 80)
+FIRST_PARTS = [(0, 256), (256, 256), (512, 512)]
+HALVES = [(0, 512), (512, 512)]
 CHUNKS0 = [(0, 512), (512, 512), (1024, 512), (1536, 512)]
 CHUNKS1 = [(0, 512), (512, 512), (1024, 512), (1536, 256), (1792, 128), (1920, 128)]
 
 AT_PAGE, AT_VCODES, AT_WCODES, AT_Y = 0, 24, (179, 36), 24
 AT_PICKED_SC, AT_WSC, AT_CEN = 49, 50, 55.5
-AT_X, AT_ZCODES, AT_ZSC, AT_VSC = (84, 56, 60), (128, 64), 72, 80
+AT_X, AT_ZCODES, AT_ZSC, AT_VSC = (84, 56, 60), (132, 64), 72, 80
 AT_WGS, AT_WGO = (76, 96, 100), 76
 AT_W4, AT_W4SC, AT_STAGE, AT_DESK = 140, 141.5, 143, 145
 AT_TAB, AT_RAW0, AT_TABSC = (108, 124, 155), (171, 187, 195), 203
 AT_H = 84
-AT_HS = (114, 126, 132, 203, 108, 116, 124, 128)
-BED0_PIECES = ((0, 0, 1024), (0, 1024, 1024), (1, 0, 512), (1, 512, 512), (1, 1024, 1024))
+AT_HS = (203, 207, 211, 215, 124, 128, 132, 136)
+BED0_PIECES = ((0, 0, 2048), (1, 0, 2048), (2, 0, 1024), (2, 1024, 1024), (3, 0, 1024), (3, 1024, 1024))
 AT_RAW1, AT_CLOSE, AT_BED0, AT_BED1, AT_Z0 = 155, 155, 108, 203, 187
-PAIR_COLS = 256
 
 
 def tile_list_bed_request_matching_kernel(
@@ -51,7 +52,12 @@ def tile_list_bed_request_matching_kernel(
     with ExitStack() as ctx:
         lists = ctx.enter_context(tc.tile_pool(name="lists", bufs=1))
         keep = ctx.enter_context(tc.tile_pool(name="keep", bufs=1))
-        psum = ctx.enter_context(tc.psum_pool(name="psum", bufs=4))
+        psum = ctx.enter_context(tc.psum_pool(name="psum", bufs=1))
+        banks = []
+
+        def bank(number):
+            banks.append(psum.tile([P, BANK], F32, name="acc%d" % len(banks), offset=number * 2 * KIB))
+            return banks[-1]
 
         def sb(shape, dtype, name, at):
             return keep.tile(shape, dtype, name=name, tag=name, align_bytes=64, offset=int(at * KIB))
@@ -152,41 +158,43 @@ def tile_list_bed_request_matching_kernel(
             rounded = staging("w0r%d" % a, a)
             round_w1(rounded[:], raw0[a][:])
             quantise_w1(0, a, a + 1, rounded[:])
-        gather_table(2, 0, BANK)
-        gather_table(2, BANK, S)
+        for lo, width in HALVES:
+            gather_table(2, lo, lo + width)
 
         raw1 = sb([P, PASS1, 4, KP], F32, "raw1", AT_RAW1)
-        for a in range(PASS1):
-            load_w1(raw1[:, a, :, :], a, 1)
+        load_w1(raw1[:, 0, :, :], 0, 1)
         wgs_sb.extend(load_wgs(2, 4))
+        load_w1(raw1[:, 1, :, :], 1, 1)
+        load_w1(raw1[:, 2, :, :], 2, 1)
+        bed0 = [load_bed(0, t, t + 1, lo, width, AT_BED0 + 8 * t + lo // 256) for t, lo, width in BED0_PIECES]
 
         def distances(step):
             b, t = divmod(step, 4)
             h = sb([P, S], F32, "h%d" % step, AT_H + 4 * (step % 3))
             placed = sb([P, S], F32, "placed%d" % step, AT_HS[step])
-            for lo in range(0, S, BANK):
-                acc = psum.tile([P, BANK], F32, name="acc1", tag="acc1")
+            for lo, width in FIRST_PARTS if step == 0 else HALVES:
+                acc = bank(len(banks) % 4)
                 for a in range(PASS1):
                     cols = slice(a * KP + t * P, a * KP + (t + 1) * P)
                     nc.tensor.matmul_mx(
-                        acc[:],
+                        acc[:, 0:width],
                         lhsT=w_codes[b][:, cols].bitcast(FP8X4),
                         lhsT_scale=w_sc[b][:, cols],
-                        rhs=v_codes[a][:, lo:lo + BANK].bitcast(FP8X4),
-                        rhs_scale=v_sc[:, a * S + lo:a * S + lo + BANK],
+                        rhs=v_codes[a][:, lo:lo + width].bitcast(FP8X4),
+                        rhs_scale=v_sc[:, a * S + lo:a * S + lo + width],
                         start=(a == 0), stop=(a == PASS1 - 1),
                     )
-                part = h[:, lo:lo + BANK]
-                nc.scalar.activation(part, acc[:], ACT.Square, bias=cen[:, b, t:t + 1], scale=-1.0)
-                nc.gpsimd.tensor_tensor(placed[:, lo:lo + BANK], part, wgs_sb[t][:, lo:lo + BANK], MULT)
+                part = h[:, lo:lo + width]
+                nc.scalar.activation(part, acc[:, 0:width], ACT.Square, bias=cen[:, b, t:t + 1], scale=-1.0)
+                nc.gpsimd.tensor_tensor(placed[:, lo:lo + width], part, wgs_sb[t][:, lo:lo + width], MULT)
             return placed
 
         def place(step, lo=0, hi=S):
             nc.vector.tensor_copy(pages[step % PAGES][:].indirect(idx2[:, lo // 16:hi // 16]), hs[step][:, lo:hi])
 
         hs = [distances(step) for step in range(4)]
-        place(0, 0, BANK)
-        place(0, BANK, S)
+        for lo, width in FIRST_PARTS:
+            place(0, lo, lo + width)
         place(1)
 
         rounded = staging("w1r0", 0)
@@ -198,10 +206,6 @@ def tile_list_bed_request_matching_kernel(
             round_w1(rounded[:, (a - 1) * 4 * KP:a * 4 * KP], raw1[:, a, :, :])
         quantise_w1(1, 1, 3, rounded[:])
 
-        bed0 = {
-            (pair, lo): load_bed(0, 2 * pair, 2 * pair + 2, lo, width, AT_BED0 + 16 * pair + lo // 128)
-            for pair, lo, width in BED0_PIECES
-        }
         w4_sb = sb([P, PASS2, 2 * N], U8, "w4_sb", AT_W4)
         nc.sync.dma_start(w4_sb[:].bitcast(I32), w4_words.bitcast(I32).rearrange("a p w -> p a w"))
         for q in QUADS:
@@ -212,59 +216,66 @@ def tile_list_bed_request_matching_kernel(
         idx3 = load_list(offs3, "idx3")
         idx4 = load_list(offs4, "idx4")
 
-        close = sb([P, 4, T2], F32, "close", AT_CLOSE)
-        z0_pairs = sb([P, 2, 2 * T2], BF16, "z0_pairs", AT_Z0)
+        z0_rows = sb([P, 4, T2], BF16, "z0_rows", AT_Z0)
         z_sc = [sb([P, T2], U8, "z_sc%d" % b, AT_ZSC + 2 * b) for b in range(PASS2)]
 
-        def closeness(step, chunks=CHUNKS0):
+        def closeness(dst, step, chunks=CHUNKS0):
             for lo, width in chunks:
-                nc.scalar.activation(
-                    close[:, step % 4, lo:lo + width], pages[step % PAGES][:, lo:lo + width], ACT.Exp, scale=-1.0
-                )
+                nc.scalar.activation(dst[:, lo:lo + width], pages[step % PAGES][:, lo:lo + width], ACT.Exp, scale=-1.0)
 
-        def weigh_pair(piece):
-            pair, first, width = BED0_PIECES[piece]
-            rows = slice(2 * pair, 2 * pair + 2)
-            for lo in range(first, first + width, PAIR_COLS):
-                cols = slice(lo, lo + PAIR_COLS)
+        close0 = []
+
+        def closeness0(t):
+            places = [AT_CLOSE + 8 * ((t + 3) % 4) + 2 * i for i in range(4)]
+            if t == 0:
+                places[3] = AT_CLOSE + 22
+            if t == 3:
+                places = [AT_X[1] + 2 * i for i in range(4)]
+            close0.append([sb([P, BANK], F32, "close0_%d_%d" % (t, i), at) for i, at in enumerate(places)])
+            for i, dst in enumerate(close0[t]):
+                nc.scalar.activation(dst[:], pages[t % PAGES][:, i * BANK:(i + 1) * BANK], ACT.Exp, scale=-1.0)
+
+        def weigh_piece(piece):
+            t, first, width = BED0_PIECES[piece]
+            for lo in range(first, first + width, BANK):
                 nc.gpsimd.tensor_tensor(
-                    z0_pairs[:, pair, :].rearrange("p (c t) -> p c t", t=2)[:, cols, :],
-                    close[:, rows, cols].rearrange("p t c -> p c t"),
-                    bed0[(pair, first)][:, :, lo - first:lo - first + PAIR_COLS].rearrange("p t c -> p c t"),
-                    MULT,
+                    z0_rows[:, t, lo:lo + BANK], close0[t][lo // BANK][:],
+                    bed0[piece][:, 0, lo - first:lo - first + BANK], MULT,
                 )
 
-        closeness(0)
-        closeness(1)
-        weigh_pair(0)
+        closeness0(0)
+        weigh_piece(0)
+        closeness0(1)
+        weigh_piece(1)
+        closeness0(2)
+        weigh_piece(2)
         hs.append(distances(4))
         place(3)
         bed1 = load_bed(1, 0, 4, 0, T2, AT_BED1)
-        closeness(2)
-        weigh_pair(1)
+        weigh_piece(3)
         hs.append(distances(5))
         place(4)
         wgo_sb = sb([P, PK], F32, "wgo_sb", AT_WGO)
         nc.sync.dma_start(wgo_sb[:], wgo)
-        closeness(3)
-        weigh_pair(2)
+        closeness0(3)
+        weigh_piece(4)
         hs.append(distances(6))
         place(5)
-        weigh_pair(3)
+        weigh_piece(5)
         hs.append(distances(7))
-        closeness(4)
-        weigh_pair(4)
+        close = sb([P, 4, T2], F32, "close", AT_CLOSE)
+        closeness(close[:, 0, :], 4)
+        place(6)
+        closeness(close[:, 1, :], 5)
         z0 = sb([P, 4 * T2], BF16, "z0", AT_VCODES)
         for lo in range(0, T2, BANK):
             nc.scalar.copy(
-                z0[:, 4 * lo:4 * (lo + BANK)].bitcast(U32).rearrange("p (c u) -> p c u", u=2),
-                z0_pairs[:].bitcast(U32)[:, :, lo:lo + BANK].rearrange("p u c -> p c u"),
+                z0[:, 4 * lo:4 * (lo + BANK)].rearrange("p (c i t) -> p c t i", i=4, t=4),
+                z0_rows[:, :, lo:lo + BANK].rearrange("p t (c i) -> p c t i", i=4),
             )
-        place(6)
-        closeness(5)
         place(7)
-        closeness(6)
-        closeness(7, CHUNKS1)
+        closeness(close[:, 2, :], 6)
+        closeness(close[:, 3, :], 7, CHUNKS1)
 
         z_codes = [sb([P, T2], U32, "z_codes%d" % b, AT_ZCODES[b]) for b in range(PASS2)]
         ys = [sb([P, T2], F32, "y%d" % n, AT_Y + 8 * n) for n in range(NT)]
@@ -280,26 +291,44 @@ def tile_list_bed_request_matching_kernel(
             )
             return tile
 
+        sums = {}
+
+        def feature_pass(n, b, lo, width, last):
+            group = (lo // BANK, n)
+            if b == 0:
+                sums[group] = bank((4 + len(sums)) % 8)
+            at = lo % BANK
+            nc.tensor.matmul_mx(
+                sums[group][:, at:at + width],
+                lhsT=w4_sb[:, b, 2 * n * P:2 * (n + 1) * P].bitcast(FP4X4),
+                lhsT_scale=w4_sc[:, b, n * P:(n + 1) * P],
+                rhs=z_codes[b][:, lo:lo + width].bitcast(FP8X4),
+                rhs_scale=z_sc[b][:, lo:lo + width],
+                start=(b == 0), stop=last,
+            )
+
+        groups = [(c, n) for c in range(T2 // BANK) for n in range(NT)]
+
+        def open_groups(count):
+            for c, n in groups[len(sums):count]:
+                feature_pass(n, 0, c * BANK, BANK, False)
+
         def features(lo, width):
             step = BANK if width == BANK else P
+            closing = (lo + width) % BANK == 0
             for n in range(NT):
-                acc = psum.tile([P, BANK], F32, name="acc2", tag="acc2")
-                for at in range(0, width, step):
-                    cols = slice(lo + at, lo + at + step)
-                    for b in range(PASS2):
-                        nc.tensor.matmul_mx(
-                            acc[:, at:at + step],
-                            lhsT=w4_sb[:, b, 2 * n * P:2 * (n + 1) * P].bitcast(FP4X4),
-                            lhsT_scale=w4_sc[:, b, n * P:(n + 1) * P],
-                            rhs=z_codes[b][:, cols].bitcast(FP8X4),
-                            rhs_scale=z_sc[b][:, cols],
-                            start=(b == 0), stop=(b == PASS2 - 1),
-                        )
-                nc.scalar.copy(ys[n][:, lo:lo + width], acc[:, 0:width])
+                for at in range(lo, lo + width, step):
+                    feature_pass(n, 1, at, step, closing and at + step == lo + width)
+                if closing:
+                    first = lo + width - BANK
+                    nc.scalar.copy(ys[n][:, first:first + BANK], sums[(first // BANK, n)][:])
+            if closing:
+                open_groups(len(sums) + NT)
 
         for lo in range(0, T2, T2 // 2):
             cols = slice(lo, lo + T2 // 2)
             quantise(z_codes[0][:, cols], z_sc[0][:, cols], z0[:, 4 * lo:4 * lo + 2 * T2])
+        open_groups(8)
         waiting = None
         for i, chunk in enumerate(CHUNKS1 + [None]):
             made = (chunk, weigh(i, *chunk)) if chunk else None

@@ -30,16 +30,16 @@ SCALE_ROW0 = (0, 16, 80)
 FIRST_PARTS = [(0, 256), (256, 256), (512, 512)]
 HALVES = [(0, 512), (512, 512)]
 CHUNKS0 = [(0, 512), (512, 512), (1024, 512), (1536, 512)]
-CHUNKS1 = [(0, 512), (512, 512), (1024, 512), (1536, 256), (1792, 128), (1920, 128)]
+CHUNKS1 = [(0, 512), (512, 512), (1024, 512), (1536, 256), (1792, 256)]
 
 AT_PAGE, AT_VCODES, AT_WCODES, AT_Y = 0, 24, (179, 36), 24
 AT_PICKED_SC, AT_WSC, AT_CEN = 49, 50, 55.5
 AT_X, AT_ZCODES, AT_ZSC, AT_VSC = (84, 56, 60), (132, 64), 72, 80
-AT_WGS, AT_WGO = (76, 96, 100), 76
+AT_WGS, AT_WGO = (76, 96, 100, 104), 76
 AT_W4, AT_W4SC, AT_STAGE, AT_DESK = 140, 141.5, 143, 145
 AT_TAB, AT_RAW0, AT_TABSC = (108, 124, 155), (171, 187, 195), 203
 AT_H = 84
-AT_HS = (203, 207, 211, 215, 124, 128, 132, 136)
+AT_HS = (203, 207, 211, 215, 116, 124, 132, 136)
 BED0_PIECES = ((0, 0, 2048), (1, 0, 2048), (2, 0, 1024), (2, 1024, 1024), (3, 0, 1024), (3, 1024, 1024))
 AT_RAW1, AT_CLOSE, AT_BED0, AT_BED1, AT_Z0 = 155, 155, 108, 203, 187
 
@@ -162,11 +162,19 @@ def tile_list_bed_request_matching_kernel(
             gather_table(2, lo, lo + width)
 
         raw1 = sb([P, PASS1, 4, KP], F32, "raw1", AT_RAW1)
+        bed0 = []
+
+        def load_bed0(count):
+            for t, lo, width in BED0_PIECES[len(bed0):count]:
+                bed0.append(load_bed(0, t, t + 1, lo, width, AT_BED0 + 8 * t + lo // 256))
+
         load_w1(raw1[:, 0, :, :], 0, 1)
-        wgs_sb.extend(load_wgs(2, 4))
+        wgs_sb.extend(load_wgs(2, 3))
+        load_bed0(1)
         load_w1(raw1[:, 1, :, :], 1, 1)
         load_w1(raw1[:, 2, :, :], 2, 1)
-        bed0 = [load_bed(0, t, t + 1, lo, width, AT_BED0 + 8 * t + lo // 256) for t, lo, width in BED0_PIECES]
+        wgs_sb.extend(load_wgs(3, 4))
+        load_bed0(len(BED0_PIECES))
 
         def distances(step):
             b, t = divmod(step, 4)
@@ -237,23 +245,25 @@ def tile_list_bed_request_matching_kernel(
 
         def weigh_piece(piece):
             t, first, width = BED0_PIECES[piece]
-            for lo in range(first, first + width, BANK):
+            step = BANK // 2 if t == 1 else BANK
+            for lo in range(first, first + width, step):
+                at = lo % BANK
                 nc.gpsimd.tensor_tensor(
-                    z0_rows[:, t, lo:lo + BANK], close0[t][lo // BANK][:],
-                    bed0[piece][:, 0, lo - first:lo - first + BANK], MULT,
+                    z0_rows[:, t, lo:lo + step], close0[t][lo // BANK][:, at:at + step],
+                    bed0[piece][:, 0, lo - first:lo - first + step], MULT,
                 )
 
         closeness0(0)
         weigh_piece(0)
         closeness0(1)
         weigh_piece(1)
-        closeness0(2)
-        weigh_piece(2)
         hs.append(distances(4))
+        closeness0(2)
         place(3)
         bed1 = load_bed(1, 0, 4, 0, T2, AT_BED1)
-        weigh_piece(3)
+        weigh_piece(2)
         hs.append(distances(5))
+        weigh_piece(3)
         place(4)
         wgo_sb = sb([P, PK], F32, "wgo_sb", AT_WGO)
         nc.sync.dma_start(wgo_sb[:], wgo)
@@ -281,7 +291,7 @@ def tile_list_bed_request_matching_kernel(
         ys = [sb([P, T2], F32, "y%d" % n, AT_Y + 8 * n) for n in range(NT)]
 
         def weigh(i, lo, width):
-            tile = staging("z1_%d" % i, i % 3)
+            tile = staging("z1_%d" % i, (i + 1) % 3)
             cols = slice(lo, lo + width)
             nc.vector.tensor_tensor(
                 tile[:, 0:4 * width].rearrange("p (c i t) -> p c t i", i=2, t=4),

@@ -34,13 +34,14 @@ CHUNKS1 = [(0, 512), (512, 512), (1024, 512), (1536, 256), (1792, 256)]
 
 AT_PAGE, AT_VCODES, AT_WCODES, AT_Y = 0, 24, (179, 36), 24
 AT_PICKED_SC, AT_WSC, AT_CEN = 49, 50, 55.5
-AT_X, AT_ZCODES, AT_ZSC, AT_VSC = (84, 56, 60), (132, 64), 72, 80
+AT_X, AT_ZCODES, AT_ZSC, AT_VSC = (84, 56, 60), (128, 64), 72, 80
 AT_WGS, AT_WGO = (76, 96, 100, 104), 76
 AT_W4, AT_W4SC, AT_STAGE, AT_DESK = 140, 141.5, 143, 145
 AT_TAB, AT_RAW0, AT_TABSC = (108, 124, 155), (171, 187, 195), 203
 AT_H = 84
-AT_HS = (203, 207, 211, 215, 116, 124, 132, 136)
-BED0_PIECES = ((0, 0, 2048), (1, 0, 2048), (2, 0, 1024), (2, 1024, 1024), (3, 0, 1024), (3, 1024, 1024))
+AT_PLACED = (203, 207, 211, 215, 108, 120, 124, 128)
+BED0_PIECES = ((0, 0, 1536), (0, 1536, 512), (1, 0, 512), (1, 512, 768), (1, 1280, 768))
+PAIR_COLS = 256
 AT_RAW1, AT_CLOSE, AT_BED0, AT_BED1, AT_Z0 = 155, 155, 108, 203, 187
 
 
@@ -106,11 +107,9 @@ def tile_list_bed_request_matching_kernel(
         nc.gpsimd.dma_start(cen[:], centre.rearrange("(b p t) -> p b t", b=PASS2, t=4))
         raw0 = [sb([P, 4, KP], F32, "raw0_%d" % a, AT_RAW0[a]) for a in range(PASS1)]
         tabs = [load_table(0)]
-        load_w1(raw0[0][:], 0, 0)
-        load_w1(raw0[1][:], 1, 0)
-        tabs.append(load_table(1))
-        load_w1(raw0[2][:], 2, 0)
-        tabs.append(load_table(2))
+        for a in range(PASS1):
+            load_w1(raw0[a][:], a, 0)
+        tabs.extend([load_table(a) for a in range(1, PASS1)])
 
         v_codes = [sb([P, S], U32, "v_codes%d" % a, AT_VCODES + 4 * a) for a in range(PASS1)]
         w_codes = [sb([P, PASS1 * KP], U32, "w_codes%d" % b, AT_WCODES[b]) for b in range(PASS2)]
@@ -153,11 +152,10 @@ def tile_list_bed_request_matching_kernel(
         w4_sc = sb([P, PASS2, N], U8, "w4_sc", AT_W4SC)
         nc.vector.memset(w4_sc[:].rearrange("p a c -> p (a c)").bitcast(I32), 0)
         for a in range(PASS1):
-            if a == PASS1 - 1:
-                gather_table(1, 0, S)
             rounded = staging("w0r%d" % a, a)
             round_w1(rounded[:], raw0[a][:])
             quantise_w1(0, a, a + 1, rounded[:])
+        gather_table(1, 0, S)
         for lo, width in HALVES:
             gather_table(2, lo, lo + width)
 
@@ -165,13 +163,12 @@ def tile_list_bed_request_matching_kernel(
         bed0 = []
 
         def load_bed0(count):
-            for t, lo, width in BED0_PIECES[len(bed0):count]:
-                bed0.append(load_bed(0, t, t + 1, lo, width, AT_BED0 + 8 * t + lo // 256))
+            for pair, lo, width in BED0_PIECES[len(bed0):count]:
+                bed0.append(load_bed(0, 2 * pair, 2 * pair + 2, lo, width, AT_BED0 + 16 * pair + lo // 128))
 
         load_w1(raw1[:, 0, :, :], 0, 1)
-        wgs_sb.extend(load_wgs(2, 3))
-        load_bed0(1)
         load_w1(raw1[:, 1, :, :], 1, 1)
+        wgs_sb.extend(load_wgs(2, 3))
         load_w1(raw1[:, 2, :, :], 2, 1)
         wgs_sb.extend(load_wgs(3, 4))
         load_bed0(len(BED0_PIECES))
@@ -179,7 +176,7 @@ def tile_list_bed_request_matching_kernel(
         def distances(step):
             b, t = divmod(step, 4)
             h = sb([P, S], F32, "h%d" % step, AT_H + 4 * (step % 3))
-            placed = sb([P, S], F32, "placed%d" % step, AT_HS[step])
+            placed = sb([P, S], F32, "placed%d" % step, AT_PLACED[step])
             for lo, width in FIRST_PARTS if step == 0 else HALVES:
                 acc = bank(len(banks) % 4)
                 for a in range(PASS1):
@@ -205,14 +202,14 @@ def tile_list_bed_request_matching_kernel(
             place(0, lo, lo + width)
         place(1)
 
-        rounded = staging("w1r0", 0)
-        round_w1(rounded[:], raw1[:, 0, :, :])
-        quantise_w1(1, 0, 1, rounded[:])
+        rounded = staging("w1r01", 0, 2)
+        for a in range(2):
+            round_w1(rounded[:, a * 4 * KP:(a + 1) * 4 * KP], raw1[:, a, :, :])
+        quantise_w1(1, 0, 2, rounded[:])
         place(2)
-        rounded = staging("w1r12", 1, 2)
-        for a in (1, 2):
-            round_w1(rounded[:, (a - 1) * 4 * KP:a * 4 * KP], raw1[:, a, :, :])
-        quantise_w1(1, 1, 3, rounded[:])
+        rounded = staging("w1r2", 2)
+        round_w1(rounded[:], raw1[:, 2, :, :])
+        quantise_w1(1, 2, 3, rounded[:])
 
         w4_sb = sb([P, PASS2, 2 * N], U8, "w4_sb", AT_W4)
         nc.sync.dma_start(w4_sb[:].bitcast(I32), w4_words.bitcast(I32).rearrange("a p w -> p a w"))
@@ -224,68 +221,58 @@ def tile_list_bed_request_matching_kernel(
         idx3 = load_list(offs3, "idx3")
         idx4 = load_list(offs4, "idx4")
 
-        z0_rows = sb([P, 4, T2], BF16, "z0_rows", AT_Z0)
+        close = sb([P, 4, T2], F32, "close", AT_CLOSE)
+        z0_pairs = sb([P, 2, 2 * T2], BF16, "z0_pairs", AT_Z0)
         z_sc = [sb([P, T2], U8, "z_sc%d" % b, AT_ZSC + 2 * b) for b in range(PASS2)]
 
-        def closeness(dst, step, chunks=CHUNKS0):
+        def closeness(steps, chunks=CHUNKS0):
             for lo, width in chunks:
-                nc.scalar.activation(dst[:, lo:lo + width], pages[step % PAGES][:, lo:lo + width], ACT.Exp, scale=-1.0)
+                for step in steps:
+                    nc.scalar.activation(
+                        close[:, step % 4, lo:lo + width], pages[step % PAGES][:, lo:lo + width], ACT.Exp, scale=-1.0
+                    )
 
-        close0 = []
-
-        def closeness0(t):
-            places = [AT_CLOSE + 8 * ((t + 3) % 4) + 2 * i for i in range(4)]
-            if t == 0:
-                places[3] = AT_CLOSE + 22
-            if t == 3:
-                places = [AT_X[1] + 2 * i for i in range(4)]
-            close0.append([sb([P, BANK], F32, "close0_%d_%d" % (t, i), at) for i, at in enumerate(places)])
-            for i, dst in enumerate(close0[t]):
-                nc.scalar.activation(dst[:], pages[t % PAGES][:, i * BANK:(i + 1) * BANK], ACT.Exp, scale=-1.0)
-
-        def weigh_piece(piece):
-            t, first, width = BED0_PIECES[piece]
-            step = BANK // 2 if t == 1 else BANK
-            for lo in range(first, first + width, step):
-                at = lo % BANK
+        def weigh_pair(piece):
+            pair, first, width = BED0_PIECES[piece]
+            for lo in range(first, first + width, PAIR_COLS):
+                cols = slice(lo, lo + PAIR_COLS)
                 nc.gpsimd.tensor_tensor(
-                    z0_rows[:, t, lo:lo + step], close0[t][lo // BANK][:, at:at + step],
-                    bed0[piece][:, 0, lo - first:lo - first + step], MULT,
+                    z0_pairs[:, pair, :].rearrange("p (c t) -> p c t", t=2)[:, cols, :],
+                    close[:, 2 * pair:2 * pair + 2, cols].rearrange("p t c -> p c t"),
+                    bed0[piece][:, :, lo - first:lo - first + PAIR_COLS].rearrange("p t c -> p c t"),
+                    MULT,
                 )
 
-        closeness0(0)
-        weigh_piece(0)
-        closeness0(1)
-        weigh_piece(1)
+        closeness([0, 1])
+        weigh_pair(0)
         hs.append(distances(4))
-        closeness0(2)
         place(3)
         bed1 = load_bed(1, 0, 4, 0, T2, AT_BED1)
-        weigh_piece(2)
+        closeness([2])
+        weigh_pair(1)
         hs.append(distances(5))
-        weigh_piece(3)
         place(4)
         wgo_sb = sb([P, PK], F32, "wgo_sb", AT_WGO)
         nc.sync.dma_start(wgo_sb[:], wgo)
-        closeness0(3)
-        weigh_piece(4)
+        closeness([3])
+        weigh_pair(2)
         hs.append(distances(6))
         place(5)
-        weigh_piece(5)
+        weigh_pair(3)
         hs.append(distances(7))
-        close = sb([P, 4, T2], F32, "close", AT_CLOSE)
-        closeness(close[:, 0, :], 4)
-        place(6)
-        closeness(close[:, 1, :], 5)
+        closeness([4])
+        weigh_pair(4)
         z0 = sb([P, 4 * T2], BF16, "z0", AT_VCODES)
         for lo in range(0, T2, BANK):
             nc.scalar.copy(
-                z0[:, 4 * lo:4 * (lo + BANK)].rearrange("p (c i t) -> p c t i", i=4, t=4),
-                z0_rows[:, :, lo:lo + BANK].rearrange("p t (c i) -> p c t i", i=4),
+                z0[:, 4 * lo:4 * (lo + BANK)].bitcast(U32).rearrange("p (c u) -> p c u", u=2),
+                z0_pairs[:].bitcast(U32)[:, :, lo:lo + BANK].rearrange("p u c -> p c u"),
             )
+        place(6)
+        closeness([5])
         place(7)
-        closeness(close[:, 2, :], 6)
-        closeness(close[:, 3, :], 7, CHUNKS1)
+        closeness([6])
+        closeness([7], CHUNKS1)
 
         z_codes = [sb([P, T2], U32, "z_codes%d" % b, AT_ZCODES[b]) for b in range(PASS2)]
         ys = [sb([P, T2], F32, "y%d" % n, AT_Y + 8 * n) for n in range(NT)]

@@ -117,8 +117,8 @@ def tile_list_bed_request_matching_kernel(
 
         def round_w1(dst, raw):
             nc.scalar.copy(
-                dst.rearrange("p (u e m j) -> p u m j e", u=2, e=2, j=4),
-                raw.rearrange("p j (m u e) -> p u m j e", u=2, e=2),
+                dst.rearrange("p (u e m j) -> p u m e j", u=2, e=2, j=4),
+                raw.rearrange("p j (m u e) -> p u m e j", u=2, e=2),
             )
 
         def quantise(codes, scales, src):

@@ -15,6 +15,7 @@ FP8X4 = mybir.dt.float8_e4m3fn_x4
 FP4X4 = mybir.dt.float4_e2m1fn_x4
 ACT = mybir.ActivationFunctionType
 MULT = mybir.AluOpType.mult
+ADD = mybir.AluOpType.add
 
 P = 128
 KP = 512
@@ -34,14 +35,13 @@ CHUNKS1 = [(0, 512), (512, 512), (1024, 512), (1536, 256), (1792, 256)]
 
 AT_PAGE, AT_VCODES, AT_WCODES, AT_Y = 0, 24, (179, 36), 24
 AT_PICKED_SC, AT_WSC, AT_CEN = 49, 50, 55.5
-AT_X, AT_ZCODES, AT_ZSC, AT_VSC = (84, 56, 60), (128, 64), 72, 80
+AT_X, AT_ZCODES, AT_ZSC, AT_VSC = (84, 56, 60), (120, 64), 72, 80
 AT_WGS, AT_WGO = (76, 96, 100, 104), 76
 AT_W4, AT_W4SC, AT_STAGE, AT_DESK = 140, 141.5, 143, 145
 AT_TAB, AT_RAW0, AT_TABSC = (108, 124, 155), (171, 187, 195), 203
 AT_H = 84
-AT_PLACED = (203, 207, 211, 215, 108, 120, 124, 128)
-BED0_PIECES = ((0, 0, 1536), (0, 1536, 512), (1, 0, 512), (1, 512, 768), (1, 1280, 768))
-PAIR_COLS = 256
+AT_PLACED = (203, 207, 211, 215, 108, 116, 120, 124)
+BED0_PIECES = ((0, 0, 1024), (0, 1024, 512), (0, 1536, 512), (1, 0, 1024), (1, 1024, 1024))
 AT_RAW1, AT_CLOSE, AT_BED0, AT_BED1, AT_Z0 = 155, 155, 108, 203, 187
 
 
@@ -115,11 +115,14 @@ def tile_list_bed_request_matching_kernel(
         w_codes = [sb([P, PASS1 * KP], U32, "w_codes%d" % b, AT_WCODES[b]) for b in range(PASS2)]
         w_sc = [sb([P, PASS1 * KP], U8, "w_sc%d" % b, AT_WSC + 1.5 * b) for b in range(PASS2)]
 
-        def round_w1(dst, raw):
-            nc.scalar.copy(
+        def round_views(dst, raw):
+            return (
                 dst.rearrange("p (u e m j) -> p u m e j", u=2, e=2, j=4),
                 raw.rearrange("p j (m u e) -> p u m e j", u=2, e=2),
             )
+
+        def round_on_gpsimd(dst, raw):
+            nc.gpsimd.tensor_scalar(dst, raw, 1.0, 0.0, MULT, ADD)
 
         def quantise(codes, scales, src):
             nc.vector.quantize_mx(codes.bitcast(FP8X4), scales, src)
@@ -153,7 +156,7 @@ def tile_list_bed_request_matching_kernel(
         nc.vector.memset(w4_sc[:].rearrange("p a c -> p (a c)").bitcast(I32), 0)
         for a in range(PASS1):
             rounded = staging("w0r%d" % a, a)
-            round_w1(rounded[:], raw0[a][:])
+            (nc.vector.tensor_copy if a == 1 else nc.scalar.copy)(*round_views(rounded[:], raw0[a][:]))
             quantise_w1(0, a, a + 1, rounded[:])
         gather_table(1, 0, S)
         for lo, width in HALVES:
@@ -166,10 +169,9 @@ def tile_list_bed_request_matching_kernel(
             for pair, lo, width in BED0_PIECES[len(bed0):count]:
                 bed0.append(load_bed(0, 2 * pair, 2 * pair + 2, lo, width, AT_BED0 + 16 * pair + lo // 128))
 
-        load_w1(raw1[:, 0, :, :], 0, 1)
-        load_w1(raw1[:, 1, :, :], 1, 1)
+        for a in range(PASS1):
+            load_w1(raw1[:, a, :, :], a, 1)
         wgs_sb.extend(load_wgs(2, 3))
-        load_w1(raw1[:, 2, :, :], 2, 1)
         wgs_sb.extend(load_wgs(3, 4))
         load_bed0(len(BED0_PIECES))
 
@@ -191,7 +193,10 @@ def tile_list_bed_request_matching_kernel(
                     )
                 part = h[:, lo:lo + width]
                 nc.scalar.activation(part, acc[:, 0:width], ACT.Square, bias=cen[:, b, t:t + 1], scale=-1.0)
-                nc.gpsimd.tensor_tensor(placed[:, lo:lo + width], part, wgs_sb[t][:, lo:lo + width], MULT)
+                if b == 0:
+                    nc.gpsimd.tensor_tensor(placed[:, lo:lo + width], part, wgs_sb[t][:, lo:lo + width], MULT)
+            if b == 1:
+                nc.gpsimd.tensor_tensor(placed[:], h[:], wgs_sb[t], MULT)
             return placed
 
         def place(step, lo=0, hi=S):
@@ -203,12 +208,16 @@ def tile_list_bed_request_matching_kernel(
         place(1)
 
         rounded = staging("w1r01", 0, 2)
-        for a in range(2):
-            round_w1(rounded[:, a * 4 * KP:(a + 1) * 4 * KP], raw1[:, a, :, :])
+        dst, raw = round_views(rounded[:, 0:4 * KP], raw1[:, 0, :, :])
+        for u in range(2):
+            round_on_gpsimd(dst[:, u], raw[:, u])
+        nc.scalar.copy(*round_views(rounded[:, 4 * KP:8 * KP], raw1[:, 1, :, :]))
         quantise_w1(1, 0, 2, rounded[:])
         place(2)
         rounded = staging("w1r2", 2)
-        round_w1(rounded[:], raw1[:, 2, :, :])
+        dst, raw = round_views(rounded[:], raw1[:, 2, :, :])
+        nc.scalar.copy(dst[:, 0], raw[:, 0])
+        round_on_gpsimd(dst[:, 1], raw[:, 1])
         quantise_w1(1, 2, 3, rounded[:])
 
         w4_sb = sb([P, PASS2, 2 * N], U8, "w4_sb", AT_W4)
@@ -225,21 +234,22 @@ def tile_list_bed_request_matching_kernel(
         z0_pairs = sb([P, 2, 2 * T2], BF16, "z0_pairs", AT_Z0)
         z_sc = [sb([P, T2], U8, "z_sc%d" % b, AT_ZSC + 2 * b) for b in range(PASS2)]
 
-        def closeness(steps, chunks=CHUNKS0):
+        def closeness(steps, chunks=CHUNKS0, scale=-1.0):
             for lo, width in chunks:
                 for step in steps:
                     nc.scalar.activation(
-                        close[:, step % 4, lo:lo + width], pages[step % PAGES][:, lo:lo + width], ACT.Exp, scale=-1.0
+                        close[:, step % 4, lo:lo + width], pages[step % PAGES][:, lo:lo + width], ACT.Exp, scale=scale
                     )
 
         def weigh_pair(piece):
             pair, first, width = BED0_PIECES[piece]
-            for lo in range(first, first + width, PAIR_COLS):
-                cols = slice(lo, lo + PAIR_COLS)
+            for lo in range(first, first + width, BANK):
+                hi = min(lo + BANK, first + width)
+                cols = slice(lo, hi)
                 nc.gpsimd.tensor_tensor(
                     z0_pairs[:, pair, :].rearrange("p (c t) -> p c t", t=2)[:, cols, :],
                     close[:, 2 * pair:2 * pair + 2, cols].rearrange("p t c -> p c t"),
-                    bed0[piece][:, :, lo - first:lo - first + PAIR_COLS].rearrange("p t c -> p c t"),
+                    bed0[piece][:, :, lo - first:hi - first].rearrange("p t c -> p c t"),
                     MULT,
                 )
 
@@ -254,9 +264,9 @@ def tile_list_bed_request_matching_kernel(
         place(4)
         wgo_sb = sb([P, PK], F32, "wgo_sb", AT_WGO)
         nc.sync.dma_start(wgo_sb[:], wgo)
-        closeness([3])
         weigh_pair(2)
         hs.append(distances(6))
+        closeness([3])
         place(5)
         weigh_pair(3)
         hs.append(distances(7))
@@ -272,7 +282,9 @@ def tile_list_bed_request_matching_kernel(
         closeness([5])
         place(7)
         closeness([6])
-        closeness([7], CHUNKS1)
+        minus_one = sb([P, 1], F32, "minus_one", AT_Z0)
+        nc.gpsimd.memset(minus_one[:], -1.0)
+        closeness([7], CHUNKS1, minus_one[:])
 
         z_codes = [sb([P, T2], U32, "z_codes%d" % b, AT_ZCODES[b]) for b in range(PASS2)]
         ys = [sb([P, T2], F32, "y%d" % n, AT_Y + 8 * n) for n in range(NT)]
@@ -322,13 +334,18 @@ def tile_list_bed_request_matching_kernel(
             if closing:
                 open_groups(len(sums) + NT)
 
-        for lo in range(0, T2, T2 // 2):
-            cols = slice(lo, lo + T2 // 2)
-            quantise(z_codes[0][:, cols], z_sc[0][:, cols], z0[:, 4 * lo:4 * lo + 2 * T2])
-        open_groups(8)
+        def quantise_z0(half):
+            cols = slice(half * T2 // 2, (half + 1) * T2 // 2)
+            quantise(z_codes[0][:, cols], z_sc[0][:, cols], z0[:, 4 * cols.start:4 * cols.stop])
+
+        quantise_z0(0)
+        open_groups(2 * NT)
         waiting = None
         for i, chunk in enumerate(CHUNKS1 + [None]):
             made = (chunk, weigh(i, *chunk)) if chunk else None
+            if i == 0:
+                quantise_z0(1)
+                open_groups(8)
             if waiting:
                 (lo, width), tile = waiting
                 quantise(z_codes[1][:, lo:lo + width], z_sc[1][:, lo:lo + width], tile[:, 0:4 * width])

@@ -33,16 +33,16 @@ HALVES = [(0, 512), (512, 512)]
 CHUNKS0 = [(0, 512), (512, 512), (1024, 512), (1536, 512)]
 CHUNKS1 = [(0, 512), (512, 512), (1024, 512), (1536, 256), (1792, 256)]
 
-AT_PAGE, AT_VCODES, AT_WCODES, AT_Y = 0, 24, (179, 36), 24
-AT_PICKED_SC, AT_WSC, AT_CEN = 49, 50, 55.5
+AT_PAGE, AT_VCODES, AT_WCODES, AT_Y = 0, 24, (180, 36), 24
+AT_PICKED_SC, AT_WSC, AT_CEN = 179, 50, 55.5
 AT_X, AT_ZCODES, AT_ZSC, AT_VSC = (84, 56, 60), (120, 64), 72, 80
 AT_WGS, AT_WGO = (76, 96, 100, 104), 76
 AT_W4, AT_W4SC, AT_STAGE, AT_DESK = 140, 141.5, 143, 145
-AT_TAB, AT_RAW0, AT_TABSC = (108, 124, 155), (171, 187, 195), 203
+AT_TAB, AT_RAW0, AT_TABSC = (108, 124, 155), (171, 187, 195), 16
 AT_H = 84
 AT_PLACED = (203, 207, 211, 215, 108, 116, 120, 124)
 BED0_PIECES = ((0, 0, 1024), (0, 1024, 512), (0, 1536, 512), (1, 0, 1024), (1, 1024, 1024))
-AT_RAW1, AT_CLOSE, AT_BED0, AT_BED1, AT_Z0 = 155, 155, 108, 203, 187
+AT_RAW1, AT_CLOSE, AT_BED0, AT_BED1, AT_Z0 = 156, 155, 108, 203, 187
 
 
 def tile_list_bed_request_matching_kernel(
@@ -102,7 +102,11 @@ def tile_list_bed_request_matching_kernel(
             nc.vector.memset(tab_sc[32 * q:32 * q + 32, :].bitcast(I32), 0)
         v_sc = sb([P, PASS1 * S], U8, "v_sc", AT_VSC)
         nc.vector.memset(v_sc[:].bitcast(I32), 0)
+        w4_sc = sb([P, PASS2, N], U8, "w4_sc", AT_W4SC)
+        nc.vector.memset(w4_sc[:].rearrange("p a c -> p (a c)").bitcast(I32), 0)
         pages = [sb([P, T2], F32, "page%d" % i, AT_PAGE + 8 * i) for i in range(PAGES)]
+        for tile in pages[:-1]:
+            nc.vector.memset(tile[:], 0.0)
         cen = sb([P, PASS2, 4], F32, "cen", AT_CEN)
         nc.gpsimd.dma_start(cen[:], centre.rearrange("(b p t) -> p b t", b=PASS2, t=4))
         raw0 = [sb([P, 4, KP], F32, "raw0_%d" % a, AT_RAW0[a]) for a in range(PASS1)]
@@ -148,15 +152,11 @@ def tile_list_bed_request_matching_kernel(
         idx2 = load_list(offs2, "idx2")
         wgs_sb.extend(load_wgs(1, 2))
 
-        nc.vector.memset(pages[0][:], 0.0)
+        nc.gpsimd.memset(pages[-1][:], 0.0)
         gather_table(0, 0, S)
-        for tile in pages[1:]:
-            nc.vector.memset(tile[:], 0.0)
-        w4_sc = sb([P, PASS2, N], U8, "w4_sc", AT_W4SC)
-        nc.vector.memset(w4_sc[:].rearrange("p a c -> p (a c)").bitcast(I32), 0)
         for a in range(PASS1):
             rounded = staging("w0r%d" % a, a)
-            (nc.vector.tensor_copy if a == 1 else nc.scalar.copy)(*round_views(rounded[:], raw0[a][:]))
+            nc.scalar.copy(*round_views(rounded[:], raw0[a][:]))
             quantise_w1(0, a, a + 1, rounded[:])
         gather_table(1, 0, S)
         for lo, width in HALVES:

@@ -28,19 +28,20 @@ OUTS = 2
 KIB = 1024
 QUADS = (0, 2, 1, 3)
 SCALE_ROW0 = (0, 16, 80)
+QUARTER = S // 4
 FIRST_PARTS = [(0, 256), (256, 256), (512, 512)]
 HALVES = [(0, 512), (512, 512)]
 CHUNKS0 = [(0, 512), (512, 512), (1024, 512), (1536, 512)]
 CHUNKS1 = [(0, 512), (512, 512), (1024, 512), (1536, 256), (1792, 256)]
 
-AT_PAGE, AT_VCODES, AT_WCODES, AT_Y = 0, 24, (180, 36), 24
-AT_PICKED_SC, AT_WSC, AT_CEN = 179, 50, 55.5
-AT_X, AT_ZCODES, AT_ZSC, AT_VSC = (84, 56, 60), (120, 64), 72, 80
+AT_PAGES, AT_VCODES, AT_WCODES, AT_Y = (0, 8, 48), 24, (180, 36), 24
+AT_PICKED_SC, AT_WSC, AT_CEN = 179, 42, 45
+AT_X, AT_ZCODES, AT_ZSC, AT_VSC = (84, 88, 92), (120, 132), 72, 80
 AT_WGS, AT_WGO = (76, 96, 100, 104), 76
-AT_W4, AT_W4SC, AT_STAGE, AT_DESK = 140, 141.5, 143, 145
-AT_TAB, AT_RAW0, AT_TABSC = (108, 124, 155), (171, 187, 195), 16
+AT_W4, AT_W4SC, AT_STAGE, AT_DESK = 140, 141.5, 143, (64, 56)
+AT_TAB, AT_RAW0, AT_TABSC = (108, 124, 155), (171, 187, 195), 54
 AT_H = 84
-AT_PLACED = (203, 207, 211, 215, 108, 116, 120, 124)
+AT_PLACED = (203, 207, 211, 143, 108, 116, 120, 124)
 BED0_PIECES = ((0, 0, 1024), (0, 1024, 512), (0, 1536, 512), (1, 0, 1024), (1, 1024, 1024))
 AT_RAW1, AT_CLOSE, AT_BED0, AT_BED1, AT_Z0 = 156, 155, 108, 203, 187
 
@@ -77,12 +78,11 @@ def tile_list_bed_request_matching_kernel(
             rows = w1[a * KP:(a + 1) * KP, b * KP:(b + 1) * KP]
             nc.sync.dma_start(dst, rows.rearrange("(p j) c -> p j c", j=4))
 
-        def load_wgs(t0, t1):
-            tile = sb([P, t1 - t0, S], F32, "wgs%d" % t0, AT_WGS[t0])
-            src = wgs.rearrange("(q t) j -> q t j", t=4)[:, t0:t1, :]
+        wgs_sb = [sb([P, S], F32, "wgs%d" % t, AT_WGS[t]) for t in range(4)]
+
+        def load_wgs(t):
             for q in QUADS:
-                nc.sync.dma_start(tile[32 * q:32 * q + 32, :, :], src)
-            return [tile[:, i, :] for i in range(t1 - t0)]
+                nc.sync.dma_start(wgs_sb[t][32 * q:32 * q + 32, :], wgs.rearrange("(q t) j -> q t j", t=4)[:, t, :])
 
         def load_bed(b, t0, t1, lo, width, at):
             tile = sb([P, t1 - t0, width], F32, "bed%d%d_%d" % (b, t0, lo), at)
@@ -94,6 +94,7 @@ def tile_list_bed_request_matching_kernel(
             return sb([P, slots * 4 * KP], BF16, name, AT_STAGE + 4 * slot)
 
         idx1 = load_list(offs, "idx1")
+        idx2 = load_list(offs2, "idx2")
         tab_sc = sb([P, T], U8, "tab_sc", AT_TABSC)
         scale_rows = tab_scales.rearrange("a q t -> (a q) t").bitcast(I32)
         nc.sync.dma_start(tab_sc[0:32, :].bitcast(I32), scale_rows[0:32])
@@ -104,7 +105,7 @@ def tile_list_bed_request_matching_kernel(
         nc.vector.memset(v_sc[:].bitcast(I32), 0)
         w4_sc = sb([P, PASS2, N], U8, "w4_sc", AT_W4SC)
         nc.vector.memset(w4_sc[:].rearrange("p a c -> p (a c)").bitcast(I32), 0)
-        pages = [sb([P, T2], F32, "page%d" % i, AT_PAGE + 8 * i) for i in range(PAGES)]
+        pages = [sb([P, T2], F32, "page%d" % i, AT_PAGES[i]) for i in range(PAGES)]
         for tile in pages[:-1]:
             nc.vector.memset(tile[:], 0.0)
         cen = sb([P, PASS2, 4], F32, "cen", AT_CEN)
@@ -125,8 +126,6 @@ def tile_list_bed_request_matching_kernel(
                 raw.rearrange("p j (m u e) -> p u m e j", u=2, e=2),
             )
 
-        def round_on_gpsimd(dst, raw):
-            nc.gpsimd.tensor_scalar(dst, raw, 1.0, 0.0, MULT, ADD)
 
         def quantise(codes, scales, src):
             nc.vector.quantize_mx(codes.bitcast(FP8X4), scales, src)
@@ -148,12 +147,14 @@ def tile_list_bed_request_matching_kernel(
                 (nc.sync if a == PASS1 - 1 else nc.gpsimd).dma_start(
                     v_sc[r:P:32, a * S:(a + 1) * S].bitcast(I32), picked_sc[row:row + 13:4, :].bitcast(I32)
                 )
-        wgs_sb = load_wgs(0, 1)
-        idx2 = load_list(offs2, "idx2")
-        wgs_sb.extend(load_wgs(1, 2))
+        load_wgs(0)
+        load_wgs(1)
 
+        outs = [sb([P, T2], F32, "desk%d" % i, AT_DESK[i]) for i in range(OUTS)]
         nc.gpsimd.memset(pages[-1][:], 0.0)
+        nc.gpsimd.memset(outs[1][:], 0.0)
         gather_table(0, 0, S)
+        nc.vector.memset(outs[0][:], 0.0)
         for a in range(PASS1):
             rounded = staging("w0r%d" % a, a)
             nc.scalar.copy(*round_views(rounded[:], raw0[a][:]))
@@ -171,8 +172,8 @@ def tile_list_bed_request_matching_kernel(
 
         for a in range(PASS1):
             load_w1(raw1[:, a, :, :], a, 1)
-        wgs_sb.extend(load_wgs(2, 3))
-        wgs_sb.extend(load_wgs(3, 4))
+        load_wgs(2)
+        load_wgs(3)
         load_bed0(len(BED0_PIECES))
 
         def distances(step):
@@ -193,31 +194,41 @@ def tile_list_bed_request_matching_kernel(
                     )
                 part = h[:, lo:lo + width]
                 nc.scalar.activation(part, acc[:, 0:width], ACT.Square, bias=cen[:, b, t:t + 1], scale=-1.0)
-                if b == 0:
+                if b == 0 and t > 0:
                     nc.gpsimd.tensor_tensor(placed[:, lo:lo + width], part, wgs_sb[t][:, lo:lo + width], MULT)
+            if step == 0:
+                head = FIRST_PARTS[0][1]
+                nc.vector.tensor_tensor(
+                    pages[0][:].indirect(idx2[:, 0:head // 16]), h[:, 0:head], wgs_sb[0][:, 0:head], MULT
+                )
             if b == 1:
-                nc.gpsimd.tensor_tensor(placed[:], h[:], wgs_sb[t], MULT)
-            return placed
+                nc.gpsimd.tensor_tensor(placed[:], h[:], wgs_sb[t][:], MULT)
+            return (h, placed) if step == 0 else placed
 
         def place(step, lo=0, hi=S):
             nc.vector.tensor_copy(pages[step % PAGES][:].indirect(idx2[:, lo // 16:hi // 16]), hs[step][:, lo:hi])
 
-        hs = [distances(step) for step in range(4)]
-        for lo, width in FIRST_PARTS:
-            place(0, lo, lo + width)
-        place(1)
-
-        rounded = staging("w1r01", 0, 2)
-        dst, raw = round_views(rounded[:, 0:4 * KP], raw1[:, 0, :, :])
+        hs = [distances(step) for step in range(2)]
+        rounded01 = staging("w1r01", 0, 2)
+        dst, raw = round_views(rounded01[:, 0:4 * KP], raw1[:, 0, :, :])
         for u in range(2):
-            round_on_gpsimd(dst[:, u], raw[:, u])
-        nc.scalar.copy(*round_views(rounded[:, 4 * KP:8 * KP], raw1[:, 1, :, :]))
-        quantise_w1(1, 0, 2, rounded[:])
+            nc.gpsimd.tensor_scalar(dst[:, u], raw[:, u], 1.0, 0.0, MULT, ADD)
+        hs.append(distances(2))
+        h0, hs[0] = hs[0]
+        for lo, width in FIRST_PARTS[1:]:
+            cols = slice(lo, lo + width)
+            nc.vector.tensor_tensor(hs[0][:, cols], h0[:, cols], wgs_sb[0][:, cols], MULT)
+            for at in range(lo, lo + width, QUARTER):
+                place(0, at, at + QUARTER)
+        place(1, 0, BANK)
+        place(1, BANK, S)
+
+        nc.scalar.copy(*round_views(rounded01[:, 4 * KP:8 * KP], raw1[:, 1, :, :]))
+        quantise_w1(1, 0, 2, rounded01[:])
+        hs.append(distances(3))
         place(2)
         rounded = staging("w1r2", 2)
-        dst, raw = round_views(rounded[:], raw1[:, 2, :, :])
-        nc.scalar.copy(dst[:, 0], raw[:, 0])
-        round_on_gpsimd(dst[:, 1], raw[:, 1])
+        nc.scalar.copy(*round_views(rounded[:], raw1[:, 2, :, :]))
         quantise_w1(1, 2, 3, rounded[:])
 
         w4_sb = sb([P, PASS2, 2 * N], U8, "w4_sb", AT_W4)
@@ -283,7 +294,7 @@ def tile_list_bed_request_matching_kernel(
         place(7)
         closeness([6])
         minus_one = sb([P, 1], F32, "minus_one", AT_Z0)
-        nc.gpsimd.memset(minus_one[:], -1.0)
+        nc.scalar.activation(minus_one[:], cen[:, 0, 0:1], ACT.Copy, bias=-1.0, scale=0.0)
         closeness([7], CHUNKS1, minus_one[:])
 
         z_codes = [sb([P, T2], U32, "z_codes%d" % b, AT_ZCODES[b]) for b in range(PASS2)]
@@ -352,9 +363,6 @@ def tile_list_bed_request_matching_kernel(
                 features(lo, width)
             waiting = made
 
-        outs = [sb([P, T2], F32, "desk%d" % i, AT_DESK + 8 * i) for i in range(OUTS)]
-        for tile in outs:
-            nc.gpsimd.memset(tile[:], 0.0)
         picked = []
         for n in range(NT):
             x = sb([P, PK], F32, "x%d" % n, AT_X[n])

@@ -15,7 +15,6 @@ FP8X4 = mybir.dt.float8_e4m3fn_x4
 FP4X4 = mybir.dt.float4_e2m1fn_x4
 ACT = mybir.ActivationFunctionType
 MULT = mybir.AluOpType.mult
-ADD = mybir.AluOpType.add
 
 P = 128
 KP = 512
@@ -23,27 +22,26 @@ PASS1 = K // KP
 PASS2 = H // KP
 NT = N // P
 BANK = 512
-PAGES = 3
-OUTS = 2
+CHUNKS = T2 // BANK
 KIB = 1024
 QUADS = (0, 2, 1, 3)
-SCALE_ROW0 = (0, 16, 80)
 QUARTER = S // 4
-FIRST_PARTS = [(0, 256), (256, 256), (512, 512)]
-HALVES = [(0, 512), (512, 512)]
-CHUNKS0 = [(0, 512), (512, 512), (1024, 512), (1536, 512)]
-CHUNKS1 = [(0, 512), (512, 512), (1024, 512), (1536, 256), (1792, 256)]
+HALF = S // 2
+PASS_ORDER = ((0, 1, 2), (2, 0, 1))
 
-AT_PAGES, AT_VCODES, AT_WCODES, AT_Y = (0, 8, 48), 24, (180, 36), 24
-AT_PICKED_SC, AT_WSC, AT_CEN = 179, 42, 45
-AT_X, AT_ZCODES, AT_ZSC, AT_VSC = (84, 88, 92), (120, 132), 72, 80
-AT_WGS, AT_WGO = (76, 96, 100, 104), 76
-AT_W4, AT_W4SC, AT_STAGE, AT_DESK = 140, 141.5, 143, (64, 56)
-AT_TAB, AT_RAW0, AT_TABSC = (108, 124, 155), (171, 187, 195), 54
-AT_H = 84
-AT_PLACED = (203, 207, 211, 143, 108, 116, 120, 124)
-BED0_PIECES = ((0, 0, 1024), (0, 1024, 512), (0, 1536, 512), (1, 0, 1024), (1, 1024, 1024))
-AT_RAW1, AT_CLOSE, AT_BED0, AT_BED1, AT_Z0 = 156, 155, 108, 203, 187
+AT_TAB, AT_PAGES, AT_BED67 = (7, 208, 32), (0, 8), 208
+AT_RAW0, AT_RAW1 = (48, 56, 64), (72, 80, 88)
+AT_PLACED = (48, 52, 56, 200, 52, 56, 48, 52)
+AT_H = (None, 60, 64, 68, 32, 60, 40, 72)
+AT_H0 = (235.5, 52, 204)
+AT_CLOSE = ((80, 88), 184, 32, 160, 40, 72)
+AT_WGS, AT_BED = 96, 112
+AT_TABSC, AT_VCODES, AT_WCODES, AT_VSC, AT_WSC = 23, (164, 160, 168), (172, 224), 178, (179, 180.5)
+AT_STAGE, AT_DESK = 188, (16, 24)
+AT_PAIRS0, AT_Z0, AT_CLOSE67, AT_PAIRS1, AT_Z1 = (64, 192), 160, 184, 112, 128
+AT_ZCODES, AT_ZSC = (48, 56), (204, 206)
+AT_Y, AT_X, AT_SCORE, AT_SQUARE = (32, 40, 76), (72, 92, 84), (48, 52, 56), 60
+AT_WGO, AT_W4, AT_W4SC, AT_CEN = 230, 234, 235.5, 236.5
 
 
 def tile_list_bed_request_matching_kernel(
@@ -74,58 +72,67 @@ def tile_list_bed_request_matching_kernel(
             nc.sync.dma_start(tile[:], tab_words[a].rearrange("p t i -> p (t i)").bitcast(I32))
             return tile
 
-        def load_w1(dst, a, b):
+        def load_w1(a, b, at):
+            tile = sb([P, 4, KP], F32, "raw%d_%d" % (b, a), at)
             rows = w1[a * KP:(a + 1) * KP, b * KP:(b + 1) * KP]
-            nc.sync.dma_start(dst, rows.rearrange("(p j) c -> p j c", j=4))
-
-        wgs_sb = [sb([P, S], F32, "wgs%d" % t, AT_WGS[t]) for t in range(4)]
-
-        def load_wgs(t):
-            for q in QUADS:
-                nc.sync.dma_start(wgs_sb[t][32 * q:32 * q + 32, :], wgs.rearrange("(q t) j -> q t j", t=4)[:, t, :])
-
-        def load_bed(b, t0, t1, lo, width, at):
-            tile = sb([P, t1 - t0, width], F32, "bed%d%d_%d" % (b, t0, lo), at)
-            rows = bedw[b * KP:(b + 1) * KP, lo:lo + width].rearrange("(p t) c -> p t c", t=4)
-            nc.sync.dma_start(tile[:], rows[:, t0:t1, :])
+            nc.sync.dma_start(tile[:], rows.rearrange("(p j) c -> p j c", j=4))
             return tile
 
-        def staging(name, slot, slots=1):
-            return sb([P, slots * 4 * KP], BF16, name, AT_STAGE + 4 * slot)
+        wgs_sb = [sb([P, S], F32, "wgs%d" % t, AT_WGS + 4 * t) for t in range(4)]
 
-        idx1 = load_list(offs, "idx1")
-        idx2 = load_list(offs2, "idx2")
+        def load_wgs(t, lo=0, hi=S):
+            rows = wgs.rearrange("(q t) j -> q t j", t=4)
+            for q in QUADS:
+                nc.sync.dma_start(wgs_sb[t][32 * q:32 * q + 32, lo:hi], rows[:, t, lo:hi])
+
+        def bed_rows(b):
+            return bedw[b * KP:(b + 1) * KP, :].rearrange("(p t) c -> p t c", t=4)
+
+        bed = []
+
+        def load_bed():
+            b, t = divmod(len(bed), 4)
+            bed.append(sb([P, T2], F32, "bed%d" % len(bed), AT_BED + 8 * len(bed)))
+            nc.sync.dma_start(bed[-1][:], bed_rows(b)[:, t, :])
+
         tab_sc = sb([P, T], U8, "tab_sc", AT_TABSC)
-        scale_rows = tab_scales.rearrange("a q t -> (a q) t").bitcast(I32)
-        nc.sync.dma_start(tab_sc[0:32, :].bitcast(I32), scale_rows[0:32])
-        nc.sync.dma_start(tab_sc[64:96, :].bitcast(I32), scale_rows[16:48])
-        for q in (1, 3):
-            nc.vector.memset(tab_sc[32 * q:32 * q + 32, :].bitcast(I32), 0)
-        v_sc = sb([P, PASS1 * S], U8, "v_sc", AT_VSC)
-        nc.vector.memset(v_sc[:].bitcast(I32), 0)
-        w4_sc = sb([P, PASS2, N], U8, "w4_sc", AT_W4SC)
-        nc.vector.memset(w4_sc[:].rearrange("p a c -> p (a c)").bitcast(I32), 0)
-        pages = [sb([P, T2], F32, "page%d" % i, AT_PAGES[i]) for i in range(PAGES)]
-        for tile in pages[:-1]:
-            nc.vector.memset(tile[:], 0.0)
+        nc.gpsimd.memset(tab_sc[:].bitcast(I32), 0)
+        for q in QUADS:
+            nc.gpsimd.dma_start(
+                tab_sc[32 * q:32 * q + 4 * PASS1, :].bitcast(I32), tab_scales[:, 4 * q:4 * q + 4, :].bitcast(I32)
+            )
         cen = sb([P, PASS2, 4], F32, "cen", AT_CEN)
         nc.gpsimd.dma_start(cen[:], centre.rearrange("(b p t) -> p b t", b=PASS2, t=4))
-        raw0 = [sb([P, 4, KP], F32, "raw0_%d" % a, AT_RAW0[a]) for a in range(PASS1)]
+        idx1 = load_list(offs, "idx1")
+        idx2 = load_list(offs2, "idx2")
+        load_wgs(0, 0, QUARTER)
         tabs = [load_table(0)]
-        for a in range(PASS1):
-            load_w1(raw0[a][:], a, 0)
+        raw0 = [load_w1(a, 0, AT_RAW0[a]) for a in range(PASS1)]
         tabs.extend([load_table(a) for a in range(1, PASS1)])
+        load_wgs(0, QUARTER, S)
+        for t in range(1, 4):
+            load_wgs(t)
+        raw1 = [load_w1(a, 1, AT_RAW1[a]) for a in range(PASS1)]
+        for step in range(4):
+            load_bed()
+        w4_sb = sb([P, PASS2, 2 * N], U8, "w4_sb", AT_W4)
+        nc.sync.dma_start(w4_sb[:].bitcast(I32), w4_words.bitcast(I32).rearrange("a p w -> p a w"))
+        idx3 = load_list(offs3, "idx3")
+        idx4 = load_list(offs4, "idx4")
+        for step in range(4, 6):
+            load_bed()
+        wgo_sb = sb([P, PK], F32, "wgo_sb", AT_WGO)
+        nc.sync.dma_start(wgo_sb[:], wgo)
 
-        v_codes = [sb([P, S], U32, "v_codes%d" % a, AT_VCODES + 4 * a) for a in range(PASS1)]
         w_codes = [sb([P, PASS1 * KP], U32, "w_codes%d" % b, AT_WCODES[b]) for b in range(PASS2)]
-        w_sc = [sb([P, PASS1 * KP], U8, "w_sc%d" % b, AT_WSC + 1.5 * b) for b in range(PASS2)]
+        w_sc = [sb([P, PASS1 * KP], U8, "w_sc%d" % b, AT_WSC[b]) for b in range(PASS2)]
+        v_codes = []
 
-        def round_views(dst, raw):
-            return (
+        def round_w1(dst, raw):
+            nc.scalar.copy(
                 dst.rearrange("p (u e m j) -> p u m e j", u=2, e=2, j=4),
                 raw.rearrange("p j (m u e) -> p u m e j", u=2, e=2),
             )
-
 
         def quantise(codes, scales, src):
             nc.vector.quantize_mx(codes.bitcast(FP8X4), scales, src)
@@ -134,246 +141,222 @@ def tile_list_bed_request_matching_kernel(
             cols = slice(a0 * KP, a1 * KP)
             quantise(w_codes[b][:, cols], w_sc[b][:, cols], src)
 
-        def gather_table(a, lo, hi):
-            nc.vector.tensor_copy(
-                v_codes[a][:, lo:hi], tabs[a][:].bitcast(U32).indirect(idx1[:, lo // 16:hi // 16])
-            )
-
-        picked_sc = sb([P, S], U8, "picked_sc", AT_PICKED_SC)
-        nc.vector.tensor_copy(picked_sc[:], tab_sc[:].indirect(idx1[:]))
-        for a in range(PASS1):
-            for r in range(4):
-                row = SCALE_ROW0[a] + r
-                (nc.sync if a == PASS1 - 1 else nc.gpsimd).dma_start(
-                    v_sc[r:P:32, a * S:(a + 1) * S].bitcast(I32), picked_sc[row:row + 13:4, :].bitcast(I32)
+        def gather_table(width):
+            a = len(v_codes)
+            v_codes.append(sb([P, S], U32, "v_codes%d" % a, AT_VCODES[a]))
+            for lo in range(0, S, width):
+                nc.vector.tensor_copy(
+                    v_codes[a][:, lo:lo + width], tabs[a][:].bitcast(U32).indirect(idx1[:, lo // 16:(lo + width) // 16])
                 )
-        load_wgs(0)
-        load_wgs(1)
 
-        outs = [sb([P, T2], F32, "desk%d" % i, AT_DESK[i]) for i in range(OUTS)]
-        nc.gpsimd.memset(pages[-1][:], 0.0)
-        nc.gpsimd.memset(outs[1][:], 0.0)
-        gather_table(0, 0, S)
-        nc.vector.memset(outs[0][:], 0.0)
+        gather_table(S)
+        v_sc = sb([P, S], U8, "v_sc", AT_VSC)
+        nc.vector.tensor_copy(v_sc[:], tab_sc[:].indirect(idx1[:]))
         for a in range(PASS1):
-            rounded = staging("w0r%d" % a, a)
-            nc.scalar.copy(*round_views(rounded[:], raw0[a][:]))
+            rounded = sb([P, 4 * KP], BF16, "w0r%d" % a, AT_STAGE + 4 * a)
+            round_w1(rounded[:], raw0[a][:])
             quantise_w1(0, a, a + 1, rounded[:])
-        gather_table(1, 0, S)
-        for lo, width in HALVES:
-            gather_table(2, lo, lo + width)
+        pages = [sb([P, T2], F32, "page%d" % i, AT_PAGES[i]) for i in range(2)]
+        desks = [sb([P, T2], F32, "desk%d" % i, AT_DESK[i]) for i in range(2)]
+        for tile in pages + desks:
+            nc.vector.memset(tile[:], 0.0)
+        gather_table(S)
+        gather_table(HALF)
+        bed67 = sb([P, 2, T2], F32, "bed67", AT_BED67)
+        nc.sync.dma_start(bed67[:], bed_rows(1)[:, 2:4, :])
 
-        raw1 = sb([P, PASS1, 4, KP], F32, "raw1", AT_RAW1)
-        bed0 = []
+        def distance(step, lo, width, dst):
+            b, t = divmod(step, 4)
+            acc = bank(len(banks) % (8 if b == 0 else 2))
+            order = PASS_ORDER[b]
+            for a in order:
+                cols = slice(a * KP + t * P, a * KP + (t + 1) * P)
+                nc.tensor.matmul_mx(
+                    acc[:, 0:width],
+                    lhsT=w_codes[b][:, cols].bitcast(FP8X4),
+                    lhsT_scale=w_sc[b][:, cols],
+                    rhs=v_codes[a][:, lo:lo + width].bitcast(FP8X4),
+                    rhs_scale=v_sc[4 * a:P, lo:lo + width],
+                    start=(a == order[0]), stop=(a == order[-1]),
+                )
+            nc.scalar.activation(dst, acc[:, 0:width], ACT.Square, bias=cen[:, b, t:t + 1], scale=-1.0)
 
-        def load_bed0(count):
-            for pair, lo, width in BED0_PIECES[len(bed0):count]:
-                bed0.append(load_bed(0, 2 * pair, 2 * pair + 2, lo, width, AT_BED0 + 16 * pair + lo // 128))
-
-        for a in range(PASS1):
-            load_w1(raw1[:, a, :, :], a, 1)
-        load_wgs(2)
-        load_wgs(3)
-        load_bed0(len(BED0_PIECES))
+        hs = {}
+        placed = {}
 
         def distances(step):
-            b, t = divmod(step, 4)
-            h = sb([P, S], F32, "h%d" % step, AT_H + 4 * (step % 3))
-            placed = sb([P, S], F32, "placed%d" % step, AT_PLACED[step])
-            for lo, width in FIRST_PARTS if step == 0 else HALVES:
-                acc = bank(len(banks) % 4)
-                for a in range(PASS1):
-                    cols = slice(a * KP + t * P, a * KP + (t + 1) * P)
-                    nc.tensor.matmul_mx(
-                        acc[:, 0:width],
-                        lhsT=w_codes[b][:, cols].bitcast(FP8X4),
-                        lhsT_scale=w_sc[b][:, cols],
-                        rhs=v_codes[a][:, lo:lo + width].bitcast(FP8X4),
-                        rhs_scale=v_sc[:, a * S + lo:a * S + lo + width],
-                        start=(a == 0), stop=(a == PASS1 - 1),
-                    )
-                part = h[:, lo:lo + width]
-                nc.scalar.activation(part, acc[:, 0:width], ACT.Square, bias=cen[:, b, t:t + 1], scale=-1.0)
-                if b == 0 and t > 0:
-                    nc.gpsimd.tensor_tensor(placed[:, lo:lo + width], part, wgs_sb[t][:, lo:lo + width], MULT)
-            if step == 0:
-                head = FIRST_PARTS[0][1]
-                nc.vector.tensor_tensor(
-                    pages[0][:].indirect(idx2[:, 0:head // 16]), h[:, 0:head], wgs_sb[0][:, 0:head], MULT
-                )
-            if b == 1:
-                nc.gpsimd.tensor_tensor(placed[:], h[:], wgs_sb[t][:], MULT)
-            return (h, placed) if step == 0 else placed
+            hs[step] = sb([P, S], F32, "h%d" % step, AT_H[step])
+            for lo in (0, HALF):
+                distance(step, lo, HALF, hs[step][:, lo:lo + HALF])
 
-        def place(step, lo=0, hi=S):
-            nc.vector.tensor_copy(pages[step % PAGES][:].indirect(idx2[:, lo // 16:hi // 16]), hs[step][:, lo:hi])
+        def weigh_h(step):
+            placed[step] = sb([P, S], F32, "placed%d" % step, AT_PLACED[step])
+            nc.gpsimd.tensor_tensor(placed[step][:], hs[step][:], wgs_sb[step % 4][:], MULT)
 
-        hs = [distances(step) for step in range(2)]
-        rounded01 = staging("w1r01", 0, 2)
-        dst, raw = round_views(rounded01[:, 0:4 * KP], raw1[:, 0, :, :])
-        for u in range(2):
-            nc.gpsimd.tensor_scalar(dst[:, u], raw[:, u], 1.0, 0.0, MULT, ADD)
-        hs.append(distances(2))
-        h0, hs[0] = hs[0]
-        for lo, width in FIRST_PARTS[1:]:
-            cols = slice(lo, lo + width)
-            nc.vector.tensor_tensor(hs[0][:, cols], h0[:, cols], wgs_sb[0][:, cols], MULT)
-            for at in range(lo, lo + width, QUARTER):
-                place(0, at, at + QUARTER)
-        place(1, 0, BANK)
-        place(1, BANK, S)
+        def window(step, lo, hi):
+            return pages[step % 2][:].indirect(idx2[:, lo // 16:hi // 16])
 
-        nc.scalar.copy(*round_views(rounded01[:, 4 * KP:8 * KP], raw1[:, 1, :, :]))
-        quantise_w1(1, 0, 2, rounded01[:])
-        hs.append(distances(3))
-        place(2)
-        rounded = staging("w1r2", 2)
-        nc.scalar.copy(*round_views(rounded[:], raw1[:, 2, :, :]))
-        quantise_w1(1, 2, 3, rounded[:])
+        def place(step):
+            nc.vector.tensor_copy(window(step, 0, S), placed[step][:])
 
-        w4_sb = sb([P, PASS2, 2 * N], U8, "w4_sb", AT_W4)
-        nc.sync.dma_start(w4_sb[:].bitcast(I32), w4_words.bitcast(I32).rearrange("a p w -> p a w"))
+        parts = [(0, QUARTER), (QUARTER, QUARTER), (HALF, HALF)]
+        h0 = [sb([P, width], F32, "h0_%d" % i, AT_H0[i]) for i, (lo, width) in enumerate(parts)]
+        for tile, (lo, width) in zip(h0, parts):
+            distance(0, lo, width, tile[:])
+        distances(1)
+        for tile, (lo, width) in zip(h0[:2], parts):
+            nc.vector.tensor_tensor(window(0, lo, lo + width), tile[:], wgs_sb[0][:, lo:lo + width], MULT)
+        placed0 = sb([P, HALF], F32, "placed0", AT_PLACED[0])
+        nc.vector.tensor_tensor(placed0[:], h0[2][:], wgs_sb[0][:, HALF:S], MULT)
+        nc.vector.tensor_copy(window(0, HALF, S), placed0[:])
+
+        w4_sc = sb([P, PASS2, N], U8, "w4_sc", AT_W4SC)
+        nc.gpsimd.memset(w4_sc[:].rearrange("p a c -> p (a c)").bitcast(I32), 0)
         for q in QUADS:
             nc.sync.dma_start(
                 w4_sc[32 * q:32 * q + 4, :, :].bitcast(I32),
                 w4_scales[:, 4 * q:4 * q + 4, :].bitcast(I32).rearrange("a r c -> r a c"),
             )
-        idx3 = load_list(offs3, "idx3")
-        idx4 = load_list(offs4, "idx4")
+        weigh_h(1)
+        distances(2)
+        rounded01 = sb([P, 2 * 4 * KP], BF16, "w1r01", AT_STAGE + 4)
+        rounded2 = sb([P, 4 * KP], BF16, "w1r2", AT_STAGE)
+        round_w1(rounded01[:, 0:4 * KP], raw1[0][:])
+        distances(3)
+        round_w1(rounded01[:, 4 * KP:8 * KP], raw1[1][:])
+        round_w1(rounded2[:], raw1[2][:])
+        place(1)
+        quantise_w1(1, 0, 2, rounded01[:, 0:8 * KP])
+        quantise_w1(1, 2, 3, rounded2[:])
+        weigh_h(2)
+        weigh_h(3)
 
-        close = sb([P, 4, T2], F32, "close", AT_CLOSE)
-        z0_pairs = sb([P, 2, 2 * T2], BF16, "z0_pairs", AT_Z0)
-        z_sc = [sb([P, T2], U8, "z_sc%d" % b, AT_ZSC + 2 * b) for b in range(PASS2)]
+        close = {}
 
-        def closeness(steps, chunks=CHUNKS0, scale=-1.0):
-            for lo, width in chunks:
-                for step in steps:
-                    nc.scalar.activation(
-                        close[:, step % 4, lo:lo + width], pages[step % PAGES][:, lo:lo + width], ACT.Exp, scale=scale
-                    )
+        halves = [slice(0, T2 // 2), slice(T2 // 2, T2)]
 
-        def weigh_pair(piece):
-            pair, first, width = BED0_PIECES[piece]
-            for lo in range(first, first + width, BANK):
-                hi = min(lo + BANK, first + width)
-                cols = slice(lo, hi)
-                nc.gpsimd.tensor_tensor(
-                    z0_pairs[:, pair, :].rearrange("p (c t) -> p c t", t=2)[:, cols, :],
-                    close[:, 2 * pair:2 * pair + 2, cols].rearrange("p t c -> p c t"),
-                    bed0[piece][:, :, lo - first:hi - first].rearrange("p t c -> p c t"),
-                    MULT,
-                )
+        def closeness(step):
+            tile = sb([P, T2], F32, "close%d" % step, AT_CLOSE[step])
+            nc.scalar.activation(tile[:], pages[step % 2][:], ACT.Exp, scale=-1.0)
+            close[step] = [tile[:, cols] for cols in halves] if step < 4 else tile
 
-        closeness([0, 1])
-        weigh_pair(0)
-        hs.append(distances(4))
+        close[0] = []
+        for i, cols in enumerate(halves):
+            tile = sb([P, T2 // 2], F32, "close0_%d" % i, AT_CLOSE[0][i])
+            nc.scalar.activation(tile[:], pages[0][:, cols], ACT.Exp, scale=-1.0)
+            close[0].append(tile[:])
+        closeness(1)
+        pairs0 = [sb([P, 2, T2], BF16, "pairs0_%d" % i, AT_PAIRS0[i]) for i in range(2)]
+
+        def weigh_z0(step):
+            u, e = divmod(step, 2)
+            for i, cols in enumerate(halves):
+                dst = pairs0[i][:, u, :].rearrange("p (c e) -> p c e", e=2)[:, :, e]
+                nc.gpsimd.tensor_tensor(dst, close[step][i], bed[step][:, cols], MULT)
+
+        weigh_z0(0)
+        place(2)
+        for step in range(4, 8):
+            distances(step)
+        weigh_h(4)
         place(3)
-        bed1 = load_bed(1, 0, 4, 0, T2, AT_BED1)
-        closeness([2])
-        weigh_pair(1)
-        hs.append(distances(5))
-        place(4)
-        wgo_sb = sb([P, PK], F32, "wgo_sb", AT_WGO)
-        nc.sync.dma_start(wgo_sb[:], wgo)
-        weigh_pair(2)
-        hs.append(distances(6))
-        closeness([3])
-        place(5)
-        weigh_pair(3)
-        hs.append(distances(7))
-        closeness([4])
-        weigh_pair(4)
-        z0 = sb([P, 4 * T2], BF16, "z0", AT_VCODES)
-        for lo in range(0, T2, BANK):
-            nc.scalar.copy(
-                z0[:, 4 * lo:4 * (lo + BANK)].bitcast(U32).rearrange("p (c u) -> p c u", u=2),
-                z0_pairs[:].bitcast(U32)[:, :, lo:lo + BANK].rearrange("p u c -> p c u"),
+        for step in range(1, 4):
+            if step > 1:
+                closeness(step)
+            weigh_z0(step)
+            weigh_h(step + 4)
+            if step > 1:
+                place(step + 2)
+
+        pairs1 = sb([P, 4 * T2], BF16, "pairs1", AT_PAIRS1)
+        pairs1_view = pairs1[:].rearrange("p (k u c e) -> p k u c e", k=CHUNKS, u=2, e=2)
+        for step in range(4, 6):
+            closeness(step)
+            nc.gpsimd.tensor_tensor(
+                pairs1_view[:, :, 0, :, step % 2],
+                close[step][:].rearrange("p (k c) -> p k c", k=CHUNKS),
+                bed[step][:].rearrange("p (k c) -> p k c", k=CHUNKS), MULT,
             )
-        place(6)
-        closeness([5])
-        place(7)
-        closeness([6])
-        minus_one = sb([P, 1], F32, "minus_one", AT_Z0)
-        nc.scalar.activation(minus_one[:], cen[:, 0, 0:1], ACT.Copy, bias=-1.0, scale=0.0)
-        closeness([7], CHUNKS1, minus_one[:])
+            place(step + 2)
+
+        def weave(dst, src):
+            nc.scalar.copy(dst.bitcast(U32).rearrange("p (c u) -> p c u", u=2), src.rearrange("p u c -> p c u"))
+
+        z0 = sb([P, 4 * T2], BF16, "z0", AT_Z0)
+        for k in range(CHUNKS):
+            weave(z0[:, 4 * BANK * k:4 * BANK * (k + 1)], pairs0[k // 2][:].bitcast(U32)[:, :, BANK * (k % 2):BANK * (k % 2 + 1)])
+
+        close67 = sb([P, 2, T2], F32, "close67", AT_CLOSE67)
+        nc.scalar.activation(close67[:, 0, :], pages[0][:], ACT.Exp, scale=-1.0)
+        for k in range(CHUNKS):
+            cols = slice(k * BANK, (k + 1) * BANK)
+            nc.scalar.activation(close67[:, 1, cols], pages[1][:, cols], ACT.Exp, scale=-1.0)
 
         z_codes = [sb([P, T2], U32, "z_codes%d" % b, AT_ZCODES[b]) for b in range(PASS2)]
-        ys = [sb([P, T2], F32, "y%d" % n, AT_Y + 8 * n) for n in range(NT)]
-
-        def weigh(i, lo, width):
-            tile = staging("z1_%d" % i, (i + 1) % 3)
-            cols = slice(lo, lo + width)
-            nc.vector.tensor_tensor(
-                tile[:, 0:4 * width].rearrange("p (c i t) -> p c t i", i=2, t=4),
-                close[:, :, cols].rearrange("p t (c i) -> p c t i", i=2),
-                bed1[:, :, cols].rearrange("p t (c i) -> p c t i", i=2),
-                MULT,
-            )
-            return tile
-
+        z_sc = [sb([P, T2], U8, "z_sc%d" % b, AT_ZSC[b]) for b in range(PASS2)]
         sums = {}
 
-        def feature_pass(n, b, lo, width, last):
-            group = (lo // BANK, n)
-            if b == 0:
-                sums[group] = bank((4 + len(sums)) % 8)
-            at = lo % BANK
+        def feature_pass(n, k, b):
+            first = (n, k) not in sums
+            if first:
+                sums[(n, k)] = bank((CHUNKS * n + k) % 8)
+            cols = slice(k * BANK, (k + 1) * BANK)
             nc.tensor.matmul_mx(
-                sums[group][:, at:at + width],
+                sums[(n, k)][:],
                 lhsT=w4_sb[:, b, 2 * n * P:2 * (n + 1) * P].bitcast(FP4X4),
                 lhsT_scale=w4_sc[:, b, n * P:(n + 1) * P],
-                rhs=z_codes[b][:, lo:lo + width].bitcast(FP8X4),
-                rhs_scale=z_sc[b][:, lo:lo + width],
-                start=(b == 0), stop=last,
+                rhs=z_codes[b][:, cols].bitcast(FP8X4),
+                rhs_scale=z_sc[b][:, cols],
+                start=first, stop=not first,
             )
 
-        groups = [(c, n) for c in range(T2 // BANK) for n in range(NT)]
+        def quantise_z(b, k0, k1, src):
+            cols = slice(k0 * BANK, k1 * BANK)
+            quantise(z_codes[b][:, cols], z_sc[b][:, cols], src)
+            for n in range(2):
+                for k in range(k0, k1):
+                    feature_pass(n, k, b)
 
-        def open_groups(count):
-            for c, n in groups[len(sums):count]:
-                feature_pass(n, 0, c * BANK, BANK, False)
+        z1 = []
+        for k in range(CHUNKS):
+            if k % 2 == 0:
+                quantise_z(0, k, k + 2, z0[:, 4 * BANK * k:4 * BANK * (k + 2)])
+            cols = slice(k * BANK, (k + 1) * BANK)
+            at = (2 * k + 1) * 2 * BANK
+            nc.vector.tensor_tensor(
+                pairs1[:, at:at + 2 * BANK].rearrange("p (c i e) -> p c e i", i=4, e=2),
+                close67[:, :, cols].rearrange("p e (c i) -> p c e i", i=4),
+                bed67[:, :, cols].rearrange("p e (c i) -> p c e i", i=4),
+                MULT,
+            )
+            z1.append(sb([P, 4 * BANK], BF16, "z1_%d" % k, AT_Z1 + 4 * k))
+            words = pairs1[:, 4 * BANK * k:4 * BANK * (k + 1)].bitcast(U32)
+            weave(z1[k][:], words.rearrange("p (u c) -> p u c", u=2))
+        for k in range(CHUNKS):
+            quantise_z(1, k, k + 1, z1[k][:])
 
-        def features(lo, width):
-            step = BANK if width == BANK else P
-            closing = (lo + width) % BANK == 0
-            for n in range(NT):
-                for at in range(lo, lo + width, step):
-                    feature_pass(n, 1, at, step, closing and at + step == lo + width)
-                if closing:
-                    first = lo + width - BANK
-                    nc.scalar.copy(ys[n][:, first:first + BANK], sums[(first // BANK, n)][:])
-            if closing:
-                open_groups(len(sums) + NT)
-
-        def quantise_z0(half):
-            cols = slice(half * T2 // 2, (half + 1) * T2 // 2)
-            quantise(z_codes[0][:, cols], z_sc[0][:, cols], z0[:, 4 * cols.start:4 * cols.stop])
-
-        quantise_z0(0)
-        open_groups(2 * NT)
-        waiting = None
-        for i, chunk in enumerate(CHUNKS1 + [None]):
-            made = (chunk, weigh(i, *chunk)) if chunk else None
-            if i == 0:
-                quantise_z0(1)
-                open_groups(8)
-            if waiting:
-                (lo, width), tile = waiting
-                quantise(z_codes[1][:, lo:lo + width], z_sc[1][:, lo:lo + width], tile[:, 0:4 * width])
-                features(lo, width)
-            waiting = made
+        ys = [sb([P, T2], F32, "y%d" % n, AT_Y[n]) for n in range(NT)]
+        for n in range(NT):
+            for k in range(CHUNKS):
+                if n == 2:
+                    for b in range(PASS2):
+                        feature_pass(n, k, b)
+                nc.scalar.copy(ys[n][:, k * BANK:(k + 1) * BANK], sums[(n, k)][:])
 
         picked = []
         for n in range(NT):
             x = sb([P, PK], F32, "x%d" % n, AT_X[n])
-            width = PK // 2 if n == 0 else PK
-            for lo in range(0, PK, width):
-                part = x[:, lo:lo + width]
-                nc.vector.tensor_copy(part, ys[n][:].indirect(idx3[:, lo // 16:(lo + width) // 16]))
-                nc.scalar.activation(part, part, ACT.Square)
-                nc.scalar.activation(part, part, ACT.Ln, bias=1.0)
+            nc.vector.tensor_copy(x[:], ys[n][:].indirect(idx3[:]))
             picked.append(x)
         for n in range(NT):
-            desk = outs[n % OUTS]
-            nc.vector.tensor_tensor(desk[:].indirect(idx4[:]), picked[n][:], wgo_sb[:], MULT)
+            score = sb([P, PK], F32, "score%d" % n, AT_SCORE[n])
+            desk = desks[n % 2]
+            for lo, width in parts if n == 0 else [(0, PK)]:
+                cols = slice(lo, lo + width)
+                square = sb([P, width], F32, "square%d_%d" % (n, lo), AT_SQUARE)
+                nc.scalar.activation(square[:], picked[n][:, cols], ACT.Square)
+                nc.scalar.activation(score[:, cols], square[:], ACT.Ln, bias=1.0)
+                nc.vector.tensor_tensor(
+                    desk[:].indirect(idx4[:, lo // 16:(lo + width) // 16]), score[:, cols], wgo_sb[:, cols], MULT
+                )
             nc.sync.dma_start(out[n * P:(n + 1) * P, :], desk[:])

@@ -33,15 +33,16 @@ AT_TAB, AT_PAGES, AT_BED67 = (7, 208, 32), (0, 8), 208
 AT_RAW0, AT_RAW1 = (48, 56, 64), (72, 80, 88)
 AT_PLACED = (48, 52, 56, 200, 52, 56, 48, 52)
 AT_H = (None, 60, 64, 68, 32, 60, 40, 72)
-AT_H0 = (235.5, 52, 204)
+AT_H0 = (234, 52, 204)
 AT_CLOSE = ((80, 88), 184, 32, 160, 40, 72)
 AT_WGS, AT_BED = 96, 112
-AT_TABSC, AT_VCODES, AT_WCODES, AT_VSC, AT_WSC = 23, (164, 160, 168), (172, 224), 178, (179, 180.5)
+AT_TABSC, AT_VCODES, AT_WCODES, AT_VSC, AT_WSC = 23, (164, 160, 168), (172, 224), 235, (179, 180.5)
+AT_PICKED_SC, SCALE_ROW0 = 178, (0, 16, 80)
 AT_STAGE, AT_DESK = 188, (16, 24)
 AT_PAIRS0, AT_Z0, AT_CLOSE67, AT_PAIRS1, AT_Z1 = (64, 192), 160, 184, 112, 128
 AT_ZCODES, AT_ZSC = (48, 56), (204, 206)
 AT_Y, AT_X, AT_SCORE, AT_SQUARE = (32, 40, 76), (72, 92, 84), (48, 52, 56), 60
-AT_WGO, AT_W4, AT_W4SC, AT_CEN = 230, 234, 235.5, 236.5
+AT_WGO, AT_W4, AT_W4SC, AT_CEN = 230, 182, 234, 183.5
 
 
 def tile_list_bed_request_matching_kernel(
@@ -96,19 +97,29 @@ def tile_list_bed_request_matching_kernel(
             nc.sync.dma_start(bed[-1][:], bed_rows(b)[:, t, :])
 
         tab_sc = sb([P, T], U8, "tab_sc", AT_TABSC)
-        nc.gpsimd.memset(tab_sc[:].bitcast(I32), 0)
-        for q in QUADS:
-            nc.gpsimd.dma_start(
-                tab_sc[32 * q:32 * q + 4 * PASS1, :].bitcast(I32), tab_scales[:, 4 * q:4 * q + 4, :].bitcast(I32)
-            )
+        idx1 = load_list(offs, "idx1")
+        scale_rows = tab_scales.rearrange("a q t -> (a q) t").bitcast(I32)
+        nc.sync.dma_start(tab_sc[0:32, :].bitcast(I32), scale_rows[0:32])
+        nc.sync.dma_start(tab_sc[64:96, :].bitcast(I32), scale_rows[16:48])
+        for q in (1, 3):
+            nc.vector.memset(tab_sc[32 * q:32 * q + 32, :].bitcast(I32), 0)
+        v_sc = sb([P, PASS1 * S], U8, "v_sc", AT_VSC)
+        nc.vector.memset(v_sc[:].bitcast(I32), 0)
         cen = sb([P, PASS2, 4], F32, "cen", AT_CEN)
         nc.gpsimd.dma_start(cen[:], centre.rearrange("(b p t) -> p b t", b=PASS2, t=4))
-        idx1 = load_list(offs, "idx1")
         idx2 = load_list(offs2, "idx2")
         load_wgs(0, 0, QUARTER)
         tabs = [load_table(0)]
         raw0 = [load_w1(a, 0, AT_RAW0[a]) for a in range(PASS1)]
         tabs.extend([load_table(a) for a in range(1, PASS1)])
+        picked_sc = sb([P, S], U8, "picked_sc", AT_PICKED_SC)
+        nc.vector.tensor_copy(picked_sc[:], tab_sc[:].indirect(idx1[:]))
+        for a in range(PASS1):
+            for r in range(4):
+                row = SCALE_ROW0[a] + r
+                (nc.sync if a == PASS1 - 1 else nc.gpsimd).dma_start(
+                    v_sc[r:P:32, a * S:(a + 1) * S].bitcast(I32), picked_sc[row:row + 13:4, :].bitcast(I32)
+                )
         load_wgs(0, QUARTER, S)
         for t in range(1, 4):
             load_wgs(t)
@@ -150,8 +161,6 @@ def tile_list_bed_request_matching_kernel(
                 )
 
         gather_table(S)
-        v_sc = sb([P, S], U8, "v_sc", AT_VSC)
-        nc.vector.tensor_copy(v_sc[:], tab_sc[:].indirect(idx1[:]))
         for a in range(PASS1):
             rounded = sb([P, 4 * KP], BF16, "w0r%d" % a, AT_STAGE + 4 * a)
             round_w1(rounded[:], raw0[a][:])
@@ -176,7 +185,7 @@ def tile_list_bed_request_matching_kernel(
                     lhsT=w_codes[b][:, cols].bitcast(FP8X4),
                     lhsT_scale=w_sc[b][:, cols],
                     rhs=v_codes[a][:, lo:lo + width].bitcast(FP8X4),
-                    rhs_scale=v_sc[4 * a:P, lo:lo + width],
+                    rhs_scale=v_sc[:, a * S + lo:a * S + lo + width],
                     start=(a == order[0]), stop=(a == order[-1]),
                 )
             nc.scalar.activation(dst, acc[:, 0:width], ACT.Square, bias=cen[:, b, t:t + 1], scale=-1.0)

@@ -1,6 +1,7 @@
 from contextlib import ExitStack
 
 import concourse.mybir as mybir
+from concourse.masks import make_identity
 
 K, H, N, T, S, T2, PK = 1536, 1024, 384, 4096, 1024, 2048, 1024
 FLOPS = 2 * K * H * S + 2 * H * N * T2
@@ -33,10 +34,13 @@ AT_TAB, AT_PAGES, AT_BED67 = (7, 208, 32), (0, 8), 208
 AT_RAW0, AT_RAW1 = (48, 56, 64), (72, 80, 88)
 AT_PLACED = (48, 52, 56, 200, 52, 56, 48, 52)
 AT_H = (None, 60, 64, 68, 32, 60, 40, 72)
-AT_H0 = (234, 52, 204)
-AT_CLOSE = ((80, 88), 184, 32, 160, 40, 72)
+AT_H0 = (234, 52, 192)
+AT_ROUNDED = (192, 84)
+AT_CLOSE = ((80, 92), 84, 32, 160, 40, 72)
 AT_WGS, AT_BED = 96, 112
 AT_TABSC, AT_VCODES, AT_WCODES, AT_VSC, AT_WSC = 23, (164, 160, 168), (172, 224), 235, (179, 180.5)
+AT_WGS_ROWS, AT_WGS_TURNED, AT_IDENTITY = 0, (200, 184), 206
+FIRST_BANKS = (0, 1, 2, 3, 6, 7, 4, 5, 0)
 AT_PICKED_SC, SCALE_ROW0 = 178, (0, 16, 80)
 AT_STAGE, AT_DESK = 188, (16, 24)
 AT_PAIRS0, AT_Z0, AT_CLOSE67, AT_PAIRS1, AT_Z1 = (64, 192), 160, 184, 112, 128
@@ -79,13 +83,6 @@ def tile_list_bed_request_matching_kernel(
             nc.sync.dma_start(tile[:], rows.rearrange("(p j) c -> p j c", j=4))
             return tile
 
-        wgs_sb = [sb([P, S], F32, "wgs%d" % t, AT_WGS + 4 * t) for t in range(4)]
-
-        def load_wgs(t, lo=0, hi=S):
-            rows = wgs.rearrange("(q t) j -> q t j", t=4)
-            for q in QUADS:
-                nc.sync.dma_start(wgs_sb[t][32 * q:32 * q + 32, lo:hi], rows[:, t, lo:hi])
-
         def bed_rows(b):
             return bedw[b * KP:(b + 1) * KP, :].rearrange("(p t) c -> p t c", t=4)
 
@@ -107,11 +104,13 @@ def tile_list_bed_request_matching_kernel(
         nc.vector.memset(v_sc[:].bitcast(I32), 0)
         cen = sb([P, PASS2, 4], F32, "cen", AT_CEN)
         nc.gpsimd.dma_start(cen[:], centre.rearrange("(b p t) -> p b t", b=PASS2, t=4))
-        idx2 = load_list(offs2, "idx2")
-        load_wgs(0, 0, QUARTER)
+        wgs_rows = sb([P, S], F32, "wgs_rows", AT_WGS_ROWS)
+        nc.sync.dma_start(wgs_rows[:], wgs)
         tabs = [load_table(0)]
         raw0 = [load_w1(a, 0, AT_RAW0[a]) for a in range(PASS1)]
         tabs.extend([load_table(a) for a in range(1, PASS1)])
+        idx2 = load_list(offs2, "idx2")
+        idx3 = load_list(offs3, "idx3")
         picked_sc = sb([P, S], U8, "picked_sc", AT_PICKED_SC)
         nc.vector.tensor_copy(picked_sc[:], tab_sc[:].indirect(idx1[:]))
         for a in range(PASS1):
@@ -120,20 +119,40 @@ def tile_list_bed_request_matching_kernel(
                 (nc.sync if a == PASS1 - 1 else nc.gpsimd).dma_start(
                     v_sc[r:P:32, a * S:(a + 1) * S].bitcast(I32), picked_sc[row:row + 13:4, :].bitcast(I32)
                 )
-        load_wgs(0, QUARTER, S)
-        for t in range(1, 4):
-            load_wgs(t)
         raw1 = [load_w1(a, 1, AT_RAW1[a]) for a in range(PASS1)]
         for step in range(4):
             load_bed()
         w4_sb = sb([P, PASS2, 2 * N], U8, "w4_sb", AT_W4)
         nc.sync.dma_start(w4_sb[:].bitcast(I32), w4_words.bitcast(I32).rearrange("a p w -> p a w"))
-        idx3 = load_list(offs3, "idx3")
         idx4 = load_list(offs4, "idx4")
         for step in range(4, 6):
             load_bed()
         wgo_sb = sb([P, PK], F32, "wgo_sb", AT_WGO)
         nc.sync.dma_start(wgo_sb[:], wgo)
+
+        identity = sb([P, P], F32, "identity", AT_IDENTITY)
+        make_identity(nc, identity[:])
+        by_entry = [bank(6), bank(7)]
+        for i in range(S // P):
+            nc.tensor.transpose(by_entry[i // 4][:, (i % 4) * P:(i % 4 + 1) * P], wgs_rows[:, i * P:(i + 1) * P], identity[:])
+        wgs_sb = []
+        for t in range(4):
+            turned = sb([P, S], F32, "wgs_turned%d" % t, AT_WGS_TURNED[t % 2])
+            wgs_sb.append(sb([P, S], F32, "wgs%d" % t, AT_WGS + 4 * t))
+            for half in range(2):
+                cols = slice(half * BANK, (half + 1) * BANK)
+                rows = by_entry[half][:].rearrange("p (i w t) -> p i w t", i=4, t=4)[:, :, :, t]
+                nc.scalar.copy(
+                    turned[:, cols].rearrange("p (i q w) -> p i q w", i=4, q=4),
+                    rows.unsqueeze(2).to_broadcast([P, 4, 4, 32]),
+                )
+            for half in range(2):
+                back = bank(4 + half)
+                for i in range(4):
+                    at = half * BANK + i * P
+                    nc.tensor.transpose(back[:, i * P:(i + 1) * P], turned[:, at:at + P], identity[:])
+                nc.scalar.copy(wgs_sb[t][:, half * BANK:(half + 1) * BANK], back[:])
+        first_sums = []
 
         w_codes = [sb([P, PASS1 * KP], U32, "w_codes%d" % b, AT_WCODES[b]) for b in range(PASS2)]
         w_sc = [sb([P, PASS1 * KP], U8, "w_sc%d" % b, AT_WSC[b]) for b in range(PASS2)]
@@ -176,7 +195,8 @@ def tile_list_bed_request_matching_kernel(
 
         def distance(step, lo, width, dst):
             b, t = divmod(step, 4)
-            acc = bank(len(banks) % (8 if b == 0 else 2))
+            acc = bank(FIRST_BANKS[len(first_sums)] if b == 0 else len(first_sums) % 2)
+            first_sums.append(acc)
             order = PASS_ORDER[b]
             for a in order:
                 cols = slice(a * KP + t * P, a * KP + (t + 1) * P)
@@ -228,8 +248,8 @@ def tile_list_bed_request_matching_kernel(
             )
         weigh_h(1)
         distances(2)
-        rounded01 = sb([P, 2 * 4 * KP], BF16, "w1r01", AT_STAGE + 4)
-        rounded2 = sb([P, 4 * KP], BF16, "w1r2", AT_STAGE)
+        rounded01 = sb([P, 2 * 4 * KP], BF16, "w1r01", AT_ROUNDED[0])
+        rounded2 = sb([P, 4 * KP], BF16, "w1r2", AT_ROUNDED[1])
         round_w1(rounded01[:, 0:4 * KP], raw1[0][:])
         distances(3)
         round_w1(rounded01[:, 4 * KP:8 * KP], raw1[1][:])

@@ -16,6 +16,7 @@ FP8X4 = mybir.dt.float8_e4m3fn_x4
 FP4X4 = mybir.dt.float4_e2m1fn_x4
 ACT = mybir.ActivationFunctionType
 MULT = mybir.AluOpType.mult
+ADD = mybir.AluOpType.add
 
 P = 128
 KP = 512
@@ -32,19 +33,19 @@ PASS_ORDER = ((0, 1, 2), (2, 0, 1))
 
 AT_TAB, AT_PAGES, AT_BED67 = (7, 208, 32), (0, 8), 208
 AT_RAW0, AT_RAW1 = (48, 56, 64), (72, 80, 88)
-AT_PLACED = (48, 52, 56, 200, 52, 56, 48, 52)
-AT_H = (None, 60, 64, 68, 32, 60, 40, 72)
+AT_PLACED = (48, 52, 56, 204, 52, 56, 48, 204)
+AT_H = (None, 60, 64, 200, 32, 60, 40, 72)
 AT_H0 = (234, 52, 192)
-AT_ROUNDED = (192, 84)
-AT_CLOSE = ((80, 92), 84, 32, 160, 40, 72)
+AT_ROUNDED = (192, 80)
+AT_CLOSE = (88, 76, 32, 160, 40, 72)
 AT_WGS, AT_BED = 96, 112
 AT_TABSC, AT_VCODES, AT_WCODES, AT_VSC, AT_WSC = 23, (164, 160, 168), (172, 224), 235, (179, 180.5)
 AT_WGS_ROWS, AT_WGS_TURNED, AT_IDENTITY = 0, (200, 184), 206
 FIRST_BANKS = (0, 1, 2, 3, 6, 7, 4, 5, 0)
 AT_PICKED_SC, SCALE_ROW0 = 178, (0, 16, 80)
 AT_STAGE, AT_DESK = 188, (16, 24)
-AT_PAIRS0, AT_Z0, AT_CLOSE67, AT_PAIRS1, AT_Z1 = (64, 192), 160, 184, 112, 128
-AT_ZCODES, AT_ZSC = (48, 56), (204, 206)
+AT_PAIRS0, AT_Z0, AT_CLOSE67, AT_PAIRS1, AT_Z1 = 185, 160, 184, 112, 128
+AT_ZCODES, AT_ZSC = (200, 56), (48, 50)
 AT_Y, AT_X, AT_SCORE, AT_SQUARE = (32, 40, 76), (72, 92, 84), (48, 52, 56), 60
 AT_WGO, AT_W4, AT_W4SC, AT_CEN = 230, 182, 234, 183.5
 
@@ -158,11 +159,14 @@ def tile_list_bed_request_matching_kernel(
         w_sc = [sb([P, PASS1 * KP], U8, "w_sc%d" % b, AT_WSC[b]) for b in range(PASS2)]
         v_codes = []
 
-        def round_w1(dst, raw):
-            nc.scalar.copy(
+        def round_views(dst, raw):
+            return (
                 dst.rearrange("p (u e m j) -> p u m e j", u=2, e=2, j=4),
                 raw.rearrange("p j (m u e) -> p u m e j", u=2, e=2),
             )
+
+        def round_w1(dst, raw):
+            nc.scalar.copy(*round_views(dst, raw))
 
         def quantise(codes, scales, src):
             nc.vector.quantize_mx(codes.bitcast(FP8X4), scales, src)
@@ -195,7 +199,7 @@ def tile_list_bed_request_matching_kernel(
 
         def distance(step, lo, width, dst):
             b, t = divmod(step, 4)
-            acc = bank(FIRST_BANKS[len(first_sums)] if b == 0 else len(first_sums) % 2)
+            acc = bank(FIRST_BANKS[len(first_sums)] if b == 0 else len(first_sums) % 4)
             first_sums.append(acc)
             order = PASS_ORDER[b]
             for a in order:
@@ -250,9 +254,11 @@ def tile_list_bed_request_matching_kernel(
         distances(2)
         rounded01 = sb([P, 2 * 4 * KP], BF16, "w1r01", AT_ROUNDED[0])
         rounded2 = sb([P, 4 * KP], BF16, "w1r2", AT_ROUNDED[1])
-        round_w1(rounded01[:, 0:4 * KP], raw1[0][:])
-        distances(3)
+        dst, raw = round_views(rounded01[:, 0:4 * KP], raw1[0][:])
+        for u in range(2):
+            nc.gpsimd.tensor_scalar(dst[:, u], raw[:, u], 1.0, 0.0, MULT, ADD)
         round_w1(rounded01[:, 4 * KP:8 * KP], raw1[1][:])
+        distances(3)
         round_w1(rounded2[:], raw1[2][:])
         place(1)
         quantise_w1(1, 0, 2, rounded01[:, 0:8 * KP])
@@ -262,40 +268,33 @@ def tile_list_bed_request_matching_kernel(
 
         close = {}
 
-        halves = [slice(0, T2 // 2), slice(T2 // 2, T2)]
-
         def closeness(step):
             tile = sb([P, T2], F32, "close%d" % step, AT_CLOSE[step])
             nc.scalar.activation(tile[:], pages[step % 2][:], ACT.Exp, scale=-1.0)
-            close[step] = [tile[:, cols] for cols in halves] if step < 4 else tile
+            close[step] = tile
 
-        close[0] = []
-        for i, cols in enumerate(halves):
-            tile = sb([P, T2 // 2], F32, "close0_%d" % i, AT_CLOSE[0][i])
-            nc.scalar.activation(tile[:], pages[0][:, cols], ACT.Exp, scale=-1.0)
-            close[0].append(tile[:])
+        closeness(0)
         closeness(1)
-        pairs0 = [sb([P, 2, T2], BF16, "pairs0_%d" % i, AT_PAIRS0[i]) for i in range(2)]
+        pairs0 = sb([P, 2, 2 * T2], BF16, "pairs0", AT_PAIRS0)
 
         def weigh_z0(step):
             u, e = divmod(step, 2)
-            for i, cols in enumerate(halves):
-                dst = pairs0[i][:, u, :].rearrange("p (c e) -> p c e", e=2)[:, :, e]
-                nc.gpsimd.tensor_tensor(dst, close[step][i], bed[step][:, cols], MULT)
+            dst = pairs0[:, u, :].rearrange("p (c e) -> p c e", e=2)[:, :, e]
+            nc.gpsimd.tensor_tensor(dst, close[step][:], bed[step][:], MULT)
 
         weigh_z0(0)
         place(2)
         for step in range(4, 8):
             distances(step)
         weigh_h(4)
+        weigh_z0(1)
         place(3)
-        for step in range(1, 4):
-            if step > 1:
-                closeness(step)
+        for step in range(5, 8):
+            weigh_h(step)
+        for step in range(2, 4):
+            closeness(step)
             weigh_z0(step)
-            weigh_h(step + 4)
-            if step > 1:
-                place(step + 2)
+            place(step + 2)
 
         pairs1 = sb([P, 4 * T2], BF16, "pairs1", AT_PAIRS1)
         pairs1_view = pairs1[:].rearrange("p (k u c e) -> p k u c e", k=CHUNKS, u=2, e=2)
@@ -313,7 +312,7 @@ def tile_list_bed_request_matching_kernel(
 
         z0 = sb([P, 4 * T2], BF16, "z0", AT_Z0)
         for k in range(CHUNKS):
-            weave(z0[:, 4 * BANK * k:4 * BANK * (k + 1)], pairs0[k // 2][:].bitcast(U32)[:, :, BANK * (k % 2):BANK * (k % 2 + 1)])
+            weave(z0[:, 4 * BANK * k:4 * BANK * (k + 1)], pairs0[:].bitcast(U32)[:, :, BANK * k:BANK * (k + 1)])
 
         close67 = sb([P, 2, T2], F32, "close67", AT_CLOSE67)
         nc.scalar.activation(close67[:, 0, :], pages[0][:], ACT.Exp, scale=-1.0)
@@ -328,7 +327,7 @@ def tile_list_bed_request_matching_kernel(
         def feature_pass(n, k, b):
             first = (n, k) not in sums
             if first:
-                sums[(n, k)] = bank((CHUNKS * n + k) % 8)
+                sums[(n, k)] = bank(CHUNKS * min(n, 1) + k)
             cols = slice(k * BANK, (k + 1) * BANK)
             nc.tensor.matmul_mx(
                 sums[(n, k)][:],
@@ -370,7 +369,8 @@ def tile_list_bed_request_matching_kernel(
                 if n == 2:
                     for b in range(PASS2):
                         feature_pass(n, k, b)
-                nc.scalar.copy(ys[n][:, k * BANK:(k + 1) * BANK], sums[(n, k)][:])
+                copy = nc.vector.tensor_copy if (n, k) == (0, CHUNKS - 1) else nc.scalar.copy
+                copy(ys[n][:, k * BANK:(k + 1) * BANK], sums[(n, k)][:])
 
         picked = []
         for n in range(NT):

@@ -34,10 +34,10 @@ PASS_ORDER = ((0, 1, 2), (2, 0, 1))
 AT_TAB, AT_PAGES, AT_BED67 = (7, 208, 32), (0, 8), 208
 AT_RAW0, AT_RAW1 = (48, 56, 64), (72, 80, 88)
 AT_PLACED = (48, 52, 56, 204, 52, 56, 48, 204)
-AT_H = (None, 60, 64, 200, 32, 60, 40, 72)
+AT_H = (None, 60, 64, 185, 120, 60, 40, 72)
 AT_H0 = (234, 52, 192)
 AT_ROUNDED = (192, 80)
-AT_CLOSE = (88, 76, 32, 160, 40, 72)
+AT_CLOSE = (88, 76, 92, 160, 40, 72)
 AT_WGS, AT_BED = 96, 112
 AT_TABSC, AT_VCODES, AT_WCODES, AT_VSC, AT_WSC = 23, (164, 160, 168), (172, 224), 235, (179, 180.5)
 AT_WGS_ROWS, AT_WGS_TURNED, AT_IDENTITY = 0, (200, 184), 206
@@ -87,12 +87,12 @@ def tile_list_bed_request_matching_kernel(
         def bed_rows(b):
             return bedw[b * KP:(b + 1) * KP, :].rearrange("(p t) c -> p t c", t=4)
 
-        bed = []
+        bed = {}
 
-        def load_bed():
-            b, t = divmod(len(bed), 4)
-            bed.append(sb([P, T2], F32, "bed%d" % len(bed), AT_BED + 8 * len(bed)))
-            nc.sync.dma_start(bed[-1][:], bed_rows(b)[:, t, :])
+        def load_bed(step):
+            b, t = divmod(step, 4)
+            bed[step] = sb([P, T2], F32, "bed%d" % step, AT_BED + 8 * step)
+            nc.sync.dma_start(bed[step][:], bed_rows(b)[:, t, :])
 
         tab_sc = sb([P, T], U8, "tab_sc", AT_TABSC)
         idx1 = load_list(offs, "idx1")
@@ -121,13 +121,13 @@ def tile_list_bed_request_matching_kernel(
                     v_sc[r:P:32, a * S:(a + 1) * S].bitcast(I32), picked_sc[row:row + 13:4, :].bitcast(I32)
                 )
         raw1 = [load_w1(a, 1, AT_RAW1[a]) for a in range(PASS1)]
-        for step in range(4):
-            load_bed()
+        for step in (0, 2, 3):
+            load_bed(step)
         w4_sb = sb([P, PASS2, 2 * N], U8, "w4_sb", AT_W4)
         nc.sync.dma_start(w4_sb[:].bitcast(I32), w4_words.bitcast(I32).rearrange("a p w -> p a w"))
         idx4 = load_list(offs4, "idx4")
         for step in range(4, 6):
-            load_bed()
+            load_bed(step)
         wgo_sb = sb([P, PK], F32, "wgo_sb", AT_WGO)
         nc.sync.dma_start(wgo_sb[:], wgo)
 
@@ -252,7 +252,7 @@ def tile_list_bed_request_matching_kernel(
             )
         weigh_h(1)
         distances(2)
-        rounded01 = sb([P, 2 * 4 * KP], BF16, "w1r01", AT_ROUNDED[0])
+        rounded01 = sb([P, 4 * 4 * KP], BF16, "w1r01", AT_ROUNDED[0])
         rounded2 = sb([P, 4 * KP], BF16, "w1r2", AT_ROUNDED[1])
         dst, raw = round_views(rounded01[:, 0:4 * KP], raw1[0][:])
         for u in range(2):
@@ -287,10 +287,12 @@ def tile_list_bed_request_matching_kernel(
         for step in range(4, 8):
             distances(step)
         weigh_h(4)
-        weigh_z0(1)
+        load_bed(1)
         place(3)
-        for step in range(5, 8):
+        for step in range(5, 7):
             weigh_h(step)
+        weigh_z0(1)
+        weigh_h(7)
         for step in range(2, 4):
             closeness(step)
             weigh_z0(step)

@@ -29,24 +29,25 @@ KIB = 1024
 QUADS = (0, 2, 1, 3)
 QUARTER = S // 4
 HALF = S // 2
+LEAD = 448
 PASS_ORDER = ((0, 1, 2), (2, 0, 1))
 
 AT_TAB, AT_PAGES, AT_BED67 = (7, 208, 32), (0, 8), 208
 AT_RAW0, AT_RAW1 = (48, 56, 64), (72, 80, 88)
 AT_PLACED = (48, 52, 56, 204, 52, 56, 48, 204)
 AT_H = (None, 60, 64, 185, 120, 60, 40, 72)
-AT_H0 = (234, 52, 192)
+AT_H0 = (52, 192)
 AT_ROUNDED = (192, 80)
 AT_CLOSE = (88, 76, 92, 160, 40, 72)
 AT_WGS, AT_BED = 96, 112
 AT_TABSC, AT_VCODES, AT_WCODES, AT_VSC, AT_WSC = 23, (164, 160, 168), (172, 224), 235, (179, 180.5)
-AT_WGS_ROWS, AT_WGS_TURNED, AT_IDENTITY = 0, (200, 184), 206
+AT_WGS_ROWS, AT_WGS_TURNED, AT_IDENTITY = 0, (200, 184), 234
 FIRST_BANKS = (0, 1, 2, 3, 6, 7, 4, 5, 0)
 AT_PICKED_SC, SCALE_ROW0 = 178, (0, 16, 80)
 AT_STAGE, AT_DESK = 188, (16, 24)
 AT_PAIRS0, AT_Z0, AT_CLOSE67, AT_PAIRS1, AT_Z1 = 185, 160, 184, 112, 128
-AT_ZCODES, AT_ZSC = (200, 56), (48, 50)
-AT_Y, AT_X, AT_SCORE, AT_SQUARE = (32, 40, 76), (72, 92, 84), (48, 52, 56), 60
+AT_ZCODES, AT_ZSC = ((204, None, 184), (56, 58, 60, 62)), (48, 50)
+AT_Y, AT_X, AT_SCORE, AT_SQUARE = (32, 40, 76), (72, 92, 84), (48, 52, 56), 62
 AT_WGO, AT_W4, AT_W4SC, AT_CEN = 230, 182, 234, 183.5
 
 
@@ -212,7 +213,11 @@ def tile_list_bed_request_matching_kernel(
                     rhs_scale=v_sc[:, a * S + lo:a * S + lo + width],
                     start=(a == order[0]), stop=(a == order[-1]),
                 )
-            nc.scalar.activation(dst, acc[:, 0:width], ACT.Square, bias=cen[:, b, t:t + 1], scale=-1.0)
+            at = 0
+            for piece in dst:
+                end = at + piece.shape[1]
+                nc.scalar.activation(piece, acc[:, at:end], ACT.Square, bias=cen[:, b, t:t + 1], scale=-1.0)
+                at = end
 
         hs = {}
         placed = {}
@@ -220,11 +225,14 @@ def tile_list_bed_request_matching_kernel(
         def distances(step):
             hs[step] = sb([P, S], F32, "h%d" % step, AT_H[step])
             for lo in (0, HALF):
-                distance(step, lo, HALF, hs[step][:, lo:lo + HALF])
+                distance(step, lo, HALF, [hs[step][:, lo:lo + HALF]])
 
         def weigh_h(step):
             placed[step] = sb([P, S], F32, "placed%d" % step, AT_PLACED[step])
-            nc.gpsimd.tensor_tensor(placed[step][:], hs[step][:], wgs_sb[step % 4][:], MULT)
+            width = HALF if step == 1 else S
+            for lo in range(0, S, width):
+                cols = slice(lo, lo + width)
+                nc.gpsimd.tensor_tensor(placed[step][:, cols], hs[step][:, cols], wgs_sb[step % 4][:, cols], MULT)
 
         def window(step, lo, hi):
             return pages[step % 2][:].indirect(idx2[:, lo // 16:hi // 16])
@@ -233,15 +241,16 @@ def tile_list_bed_request_matching_kernel(
             nc.vector.tensor_copy(window(step, 0, S), placed[step][:])
 
         parts = [(0, QUARTER), (QUARTER, QUARTER), (HALF, HALF)]
-        h0 = [sb([P, width], F32, "h0_%d" % i, AT_H0[i]) for i, (lo, width) in enumerate(parts)]
-        for tile, (lo, width) in zip(h0, parts):
-            distance(0, lo, width, tile[:])
+        lead = sb([P, LEAD], F32, "h0_lead", AT_H0[0])
+        rest = sb([P, S - LEAD], F32, "h0_rest", AT_H0[1])
+        distance(0, 0, QUARTER, [lead[:, 0:QUARTER]])
+        distance(0, QUARTER, QUARTER, [lead[:, QUARTER:LEAD], rest[:, 0:HALF - LEAD]])
+        distance(0, HALF, HALF, [rest[:, HALF - LEAD:S - LEAD]])
         distances(1)
-        for tile, (lo, width) in zip(h0[:2], parts):
-            nc.vector.tensor_tensor(window(0, lo, lo + width), tile[:], wgs_sb[0][:, lo:lo + width], MULT)
-        placed0 = sb([P, HALF], F32, "placed0", AT_PLACED[0])
-        nc.vector.tensor_tensor(placed0[:], h0[2][:], wgs_sb[0][:, HALF:S], MULT)
-        nc.vector.tensor_copy(window(0, HALF, S), placed0[:])
+        nc.vector.tensor_tensor(window(0, 0, LEAD), lead[:], wgs_sb[0][:, 0:LEAD], MULT)
+        placed0 = sb([P, S - LEAD], F32, "placed0", AT_PLACED[0])
+        nc.vector.tensor_tensor(placed0[:], rest[:], wgs_sb[0][:, LEAD:S], MULT)
+        nc.vector.tensor_copy(window(0, LEAD, S), placed0[:])
 
         w4_sc = sb([P, PASS2, N], U8, "w4_sc", AT_W4SC)
         nc.gpsimd.memset(w4_sc[:].rearrange("p a c -> p (a c)").bitcast(I32), 0)
@@ -252,6 +261,7 @@ def tile_list_bed_request_matching_kernel(
             )
         weigh_h(1)
         distances(2)
+        weigh_h(2)
         rounded01 = sb([P, 4 * 4 * KP], BF16, "w1r01", AT_ROUNDED[0])
         rounded2 = sb([P, 4 * KP], BF16, "w1r2", AT_ROUNDED[1])
         dst, raw = round_views(rounded01[:, 0:4 * KP], raw1[0][:])
@@ -263,7 +273,6 @@ def tile_list_bed_request_matching_kernel(
         place(1)
         quantise_w1(1, 0, 2, rounded01[:, 0:8 * KP])
         quantise_w1(1, 2, 3, rounded2[:])
-        weigh_h(2)
         weigh_h(3)
 
         close = {}
@@ -322,7 +331,7 @@ def tile_list_bed_request_matching_kernel(
             cols = slice(k * BANK, (k + 1) * BANK)
             nc.scalar.activation(close67[:, 1, cols], pages[1][:, cols], ACT.Exp, scale=-1.0)
 
-        z_codes = [sb([P, T2], U32, "z_codes%d" % b, AT_ZCODES[b]) for b in range(PASS2)]
+        z_codes = {}
         z_sc = [sb([P, T2], U8, "z_sc%d" % b, AT_ZSC[b]) for b in range(PASS2)]
         sums = {}
 
@@ -335,22 +344,25 @@ def tile_list_bed_request_matching_kernel(
                 sums[(n, k)][:],
                 lhsT=w4_sb[:, b, 2 * n * P:2 * (n + 1) * P].bitcast(FP4X4),
                 lhsT_scale=w4_sc[:, b, n * P:(n + 1) * P],
-                rhs=z_codes[b][:, cols].bitcast(FP8X4),
+                rhs=z_codes[(b, k)].bitcast(FP8X4),
                 rhs_scale=z_sc[b][:, cols],
                 start=first, stop=not first,
             )
 
         def quantise_z(b, k0, k1, src):
             cols = slice(k0 * BANK, k1 * BANK)
-            quantise(z_codes[b][:, cols], z_sc[b][:, cols], src)
+            codes = sb([P, (k1 - k0) * BANK], U32, "z_codes%d_%d" % (b, k0), AT_ZCODES[b][k0])
+            quantise(codes[:], z_sc[b][:, cols], src)
+            for k in range(k0, k1):
+                z_codes[(b, k)] = codes[:, (k - k0) * BANK:(k - k0 + 1) * BANK]
             for n in range(2):
                 for k in range(k0, k1):
                     feature_pass(n, k, b)
 
         z1 = []
         for k in range(CHUNKS):
-            if k % 2 == 0:
-                quantise_z(0, k, k + 2, z0[:, 4 * BANK * k:4 * BANK * (k + 2)])
+            if k == 0:
+                quantise_z(0, 0, 2, z0[:, 0:8 * BANK])
             cols = slice(k * BANK, (k + 1) * BANK)
             at = (2 * k + 1) * 2 * BANK
             nc.vector.tensor_tensor(
@@ -363,6 +375,8 @@ def tile_list_bed_request_matching_kernel(
             words = pairs1[:, 4 * BANK * k:4 * BANK * (k + 1)].bitcast(U32)
             weave(z1[k][:], words.rearrange("p (u c) -> p u c", u=2))
         for k in range(CHUNKS):
+            if k == 2:
+                quantise_z(0, 2, 4, z0[:, 8 * BANK:16 * BANK])
             quantise_z(1, k, k + 1, z1[k][:])
 
         ys = [sb([P, T2], F32, "y%d" % n, AT_Y[n]) for n in range(NT)]

from contextlib import ExitStack

import concourse.mybir as mybir
from concourse.masks import make_identity

K, H, N, T, S, T2, PK = 1536, 1024, 384, 4096, 1024, 2048, 1024
FLOPS = 2 * K * H * S + 2 * H * N * T2

F32 = mybir.dt.float32
BF16 = mybir.dt.bfloat16
I32 = mybir.dt.int32
U32 = mybir.dt.uint32
U16 = mybir.dt.uint16
U8 = mybir.dt.uint8
FP8X4 = mybir.dt.float8_e4m3fn_x4
FP4X4 = mybir.dt.float4_e2m1fn_x4
ACT = mybir.ActivationFunctionType
MULT = mybir.AluOpType.mult
ADD = mybir.AluOpType.add

P = 128
KP = 512
PASS1 = K // KP
PASS2 = H // KP
NT = N // P
BANK = 512
CHUNKS = T2 // BANK
KIB = 1024
QUADS = (0, 2, 1, 3)
QUARTER = S // 4
HALF = S // 2
LEAD = 448
PASS_ORDER = ((0, 1, 2), (2, 0, 1))

AT_TAB, AT_PAGES, AT_BED67 = (7, 208, 32), (0, 8), 208
AT_RAW0, AT_RAW1 = (48, 56, 64), (72, 80, 88)
AT_PLACED = (48, 52, 56, 204, 52, 56, 48, 204)
AT_H = (None, 60, 64, 185, 120, 60, 40, 72)
AT_H0 = (52, 192)
AT_ROUNDED = (192, 80)
AT_CLOSE = (88, 76, 92, 160, 40, 72)
AT_WGS, AT_BED = 96, 112
AT_TABSC, AT_VCODES, AT_WCODES, AT_VSC, AT_WSC = 23, (164, 160, 168), (172, 224), 235, (179, 180.5)
AT_WGS_ROWS, AT_WGS_TURNED, AT_IDENTITY = 0, (200, 184), 234
FIRST_BANKS = (0, 1, 2, 3, 6, 7, 4, 5, 0)
AT_PICKED_SC, SCALE_ROW0 = 178, (0, 16, 80)
AT_STAGE, AT_DESK = 188, (16, 24)
AT_PAIRS0, AT_Z0, AT_CLOSE67, AT_PAIRS1, AT_Z1 = 185, 160, 184, 112, 128
AT_ZCODES, AT_ZSC = ((204, None, 184), (56, 58, 60, 62)), (48, 50)
AT_Y, AT_X, AT_SCORE, AT_SQUARE = (32, 40, 76), (72, 92, 84), (48, 52, 56), 62
AT_WGO, AT_W4, AT_W4SC, AT_CEN = 230, 182, 234, 183.5


def tile_list_bed_request_matching_kernel(
    tc, tab_words, tab_scales, offs, w1, centre, offs2, wgs, bedw,
    w4_words, w4_scales, offs3, offs4, wgo, out,
):
    nc = tc.nc
    with ExitStack() as ctx:
        lists = ctx.enter_context(tc.tile_pool(name="lists", bufs=1))
        keep = ctx.enter_context(tc.tile_pool(name="keep", bufs=1))
        psum = ctx.enter_context(tc.psum_pool(name="psum", bufs=1))
        banks = []

        def bank(number):
            banks.append(psum.tile([P, BANK], F32, name="acc%d" % len(banks), offset=number * 2 * KIB))
            return banks[-1]

        def sb(shape, dtype, name, at):
            return keep.tile(shape, dtype, name=name, tag=name, align_bytes=64, offset=int(at * KIB))

        def load_list(src, name):
            tile = lists.tile([P, S // 16], U16, name=name)
            nc.sync.dma_start(tile[:], src)
            return tile

        def load_table(a):
            tile = sb([P, T], I32, "tab%d" % a, AT_TAB[a])
            nc.sync.dma_start(tile[:], tab_words[a].rearrange("p t i -> p (t i)").bitcast(I32))
            return tile

        def load_w1(a, b, at):
            tile = sb([P, 4, KP], F32, "raw%d_%d" % (b, a), at)
            rows = w1[a * KP:(a + 1) * KP, b * KP:(b + 1) * KP]
            nc.sync.dma_start(tile[:], rows.rearrange("(p j) c -> p j c", j=4))
            return tile

        def bed_rows(b):
            return bedw[b * KP:(b + 1) * KP, :].rearrange("(p t) c -> p t c", t=4)

        bed = {}

        def load_bed(step):
            b, t = divmod(step, 4)
            bed[step] = sb([P, T2], F32, "bed%d" % step, AT_BED + 8 * step)
            nc.sync.dma_start(bed[step][:], bed_rows(b)[:, t, :])

        tab_sc = sb([P, T], U8, "tab_sc", AT_TABSC)
        idx1 = load_list(offs, "idx1")
        scale_rows = tab_scales.rearrange("a q t -> (a q) t").bitcast(I32)
        nc.sync.dma_start(tab_sc[0:32, :].bitcast(I32), scale_rows[0:32])
        nc.sync.dma_start(tab_sc[64:96, :].bitcast(I32), scale_rows[16:48])
        for q in (1, 3):
            nc.vector.memset(tab_sc[32 * q:32 * q + 32, :].bitcast(I32), 0)
        v_sc = sb([P, PASS1 * S], U8, "v_sc", AT_VSC)
        nc.vector.memset(v_sc[:].bitcast(I32), 0)
        cen = sb([P, PASS2, 4], F32, "cen", AT_CEN)
        nc.gpsimd.dma_start(cen[:], centre.rearrange("(b p t) -> p b t", b=PASS2, t=4))
        wgs_rows = sb([P, S], F32, "wgs_rows", AT_WGS_ROWS)
        nc.sync.dma_start(wgs_rows[:], wgs)
        tabs = [load_table(0)]
        raw0 = [load_w1(a, 0, AT_RAW0[a]) for a in range(PASS1)]
        tabs.extend([load_table(a) for a in range(1, PASS1)])
        idx2 = load_list(offs2, "idx2")
        idx3 = load_list(offs3, "idx3")
        picked_sc = sb([P, S], U8, "picked_sc", AT_PICKED_SC)
        nc.vector.tensor_copy(picked_sc[:], tab_sc[:].indirect(idx1[:]))
        for a in range(PASS1):
            for r in range(4):
                row = SCALE_ROW0[a] + r
                (nc.sync if a == PASS1 - 1 else nc.gpsimd).dma_start(
                    v_sc[r:P:32, a * S:(a + 1) * S].bitcast(I32), picked_sc[row:row + 13:4, :].bitcast(I32)
                )
        raw1 = [load_w1(a, 1, AT_RAW1[a]) for a in range(PASS1)]
        for step in (0, 2, 3):
            load_bed(step)
        w4_sb = sb([P, PASS2, 2 * N], U8, "w4_sb", AT_W4)
        nc.sync.dma_start(w4_sb[:].bitcast(I32), w4_words.bitcast(I32).rearrange("a p w -> p a w"))
        idx4 = load_list(offs4, "idx4")
        for step in range(4, 6):
            load_bed(step)
        wgo_sb = sb([P, PK], F32, "wgo_sb", AT_WGO)
        nc.sync.dma_start(wgo_sb[:], wgo)

        identity = sb([P, P], F32, "identity", AT_IDENTITY)
        make_identity(nc, identity[:])
        by_entry = [bank(6), bank(7)]
        for i in range(S // P):
            nc.tensor.transpose(by_entry[i // 4][:, (i % 4) * P:(i % 4 + 1) * P], wgs_rows[:, i * P:(i + 1) * P], identity[:])
        wgs_sb = []
        for t in range(4):
            turned = sb([P, S], F32, "wgs_turned%d" % t, AT_WGS_TURNED[t % 2])
            wgs_sb.append(sb([P, S], F32, "wgs%d" % t, AT_WGS + 4 * t))
            for half in range(2):
                cols = slice(half * BANK, (half + 1) * BANK)
                rows = by_entry[half][:].rearrange("p (i w t) -> p i w t", i=4, t=4)[:, :, :, t]
                nc.scalar.copy(
                    turned[:, cols].rearrange("p (i q w) -> p i q w", i=4, q=4),
                    rows.unsqueeze(2).to_broadcast([P, 4, 4, 32]),
                )
            for half in range(2):
                back = bank(4 + half)
                for i in range(4):
                    at = half * BANK + i * P
                    nc.tensor.transpose(back[:, i * P:(i + 1) * P], turned[:, at:at + P], identity[:])
                nc.scalar.copy(wgs_sb[t][:, half * BANK:(half + 1) * BANK], back[:])
        first_sums = []

        w_codes = [sb([P, PASS1 * KP], U32, "w_codes%d" % b, AT_WCODES[b]) for b in range(PASS2)]
        w_sc = [sb([P, PASS1 * KP], U8, "w_sc%d" % b, AT_WSC[b]) for b in range(PASS2)]
        v_codes = []

        def round_views(dst, raw):
            return (
                dst.rearrange("p (u e m j) -> p u m e j", u=2, e=2, j=4),
                raw.rearrange("p j (m u e) -> p u m e j", u=2, e=2),
            )

        def round_w1(dst, raw):
            nc.scalar.copy(*round_views(dst, raw))

        def quantise(codes, scales, src):
            nc.vector.quantize_mx(codes.bitcast(FP8X4), scales, src)

        def quantise_w1(b, a0, a1, src):
            cols = slice(a0 * KP, a1 * KP)
            quantise(w_codes[b][:, cols], w_sc[b][:, cols], src)

        def gather_table(width):
            a = len(v_codes)
            v_codes.append(sb([P, S], U32, "v_codes%d" % a, AT_VCODES[a]))
            for lo in range(0, S, width):
                nc.vector.tensor_copy(
                    v_codes[a][:, lo:lo + width], tabs[a][:].bitcast(U32).indirect(idx1[:, lo // 16:(lo + width) // 16])
                )

        gather_table(S)
        for a in range(PASS1):
            rounded = sb([P, 4 * KP], BF16, "w0r%d" % a, AT_STAGE + 4 * a)
            round_w1(rounded[:], raw0[a][:])
            quantise_w1(0, a, a + 1, rounded[:])
        pages = [sb([P, T2], F32, "page%d" % i, AT_PAGES[i]) for i in range(2)]
        desks = [sb([P, T2], F32, "desk%d" % i, AT_DESK[i]) for i in range(2)]
        for tile in pages + desks:
            nc.vector.memset(tile[:], 0.0)
        gather_table(S)
        gather_table(HALF)
        bed67 = sb([P, 2, T2], F32, "bed67", AT_BED67)
        nc.sync.dma_start(bed67[:], bed_rows(1)[:, 2:4, :])

        def distance(step, lo, width, dst):
            b, t = divmod(step, 4)
            acc = bank(FIRST_BANKS[len(first_sums)] if b == 0 else len(first_sums) % 4)
            first_sums.append(acc)
            order = PASS_ORDER[b]
            for a in order:
                cols = slice(a * KP + t * P, a * KP + (t + 1) * P)
                nc.tensor.matmul_mx(
                    acc[:, 0:width],
                    lhsT=w_codes[b][:, cols].bitcast(FP8X4),
                    lhsT_scale=w_sc[b][:, cols],
                    rhs=v_codes[a][:, lo:lo + width].bitcast(FP8X4),
                    rhs_scale=v_sc[:, a * S + lo:a * S + lo + width],
                    start=(a == order[0]), stop=(a == order[-1]),
                )
            at = 0
            for piece in dst:
                end = at + piece.shape[1]
                nc.scalar.activation(piece, acc[:, at:end], ACT.Square, bias=cen[:, b, t:t + 1], scale=-1.0)
                at = end

        hs = {}
        placed = {}

        def distances(step):
            hs[step] = sb([P, S], F32, "h%d" % step, AT_H[step])
            for lo in (0, HALF):
                distance(step, lo, HALF, [hs[step][:, lo:lo + HALF]])

        def weigh_h(step):
            placed[step] = sb([P, S], F32, "placed%d" % step, AT_PLACED[step])
            width = HALF if step == 1 else S
            for lo in range(0, S, width):
                cols = slice(lo, lo + width)
                nc.gpsimd.tensor_tensor(placed[step][:, cols], hs[step][:, cols], wgs_sb[step % 4][:, cols], MULT)

        def window(step, lo, hi):
            return pages[step % 2][:].indirect(idx2[:, lo // 16:hi // 16])

        def place(step):
            nc.vector.tensor_copy(window(step, 0, S), placed[step][:])

        parts = [(0, QUARTER), (QUARTER, QUARTER), (HALF, HALF)]
        lead = sb([P, LEAD], F32, "h0_lead", AT_H0[0])
        rest = sb([P, S - LEAD], F32, "h0_rest", AT_H0[1])
        distance(0, 0, QUARTER, [lead[:, 0:QUARTER]])
        distance(0, QUARTER, QUARTER, [lead[:, QUARTER:LEAD], rest[:, 0:HALF - LEAD]])
        distance(0, HALF, HALF, [rest[:, HALF - LEAD:S - LEAD]])
        distances(1)
        nc.vector.tensor_tensor(window(0, 0, LEAD), lead[:], wgs_sb[0][:, 0:LEAD], MULT)
        placed0 = sb([P, S - LEAD], F32, "placed0", AT_PLACED[0])
        nc.vector.tensor_tensor(placed0[:], rest[:], wgs_sb[0][:, LEAD:S], MULT)
        nc.vector.tensor_copy(window(0, LEAD, S), placed0[:])

        w4_sc = sb([P, PASS2, N], U8, "w4_sc", AT_W4SC)
        nc.gpsimd.memset(w4_sc[:].rearrange("p a c -> p (a c)").bitcast(I32), 0)
        for q in QUADS:
            nc.sync.dma_start(
                w4_sc[32 * q:32 * q + 4, :, :].bitcast(I32),
                w4_scales[:, 4 * q:4 * q + 4, :].bitcast(I32).rearrange("a r c -> r a c"),
            )
        weigh_h(1)
        distances(2)
        weigh_h(2)
        rounded01 = sb([P, 4 * 4 * KP], BF16, "w1r01", AT_ROUNDED[0])
        rounded2 = sb([P, 4 * KP], BF16, "w1r2", AT_ROUNDED[1])
        dst, raw = round_views(rounded01[:, 0:4 * KP], raw1[0][:])
        for u in range(2):
            nc.gpsimd.tensor_scalar(dst[:, u], raw[:, u], 1.0, 0.0, MULT, ADD)
        round_w1(rounded01[:, 4 * KP:8 * KP], raw1[1][:])
        distances(3)
        round_w1(rounded2[:], raw1[2][:])
        place(1)
        quantise_w1(1, 0, 2, rounded01[:, 0:8 * KP])
        quantise_w1(1, 2, 3, rounded2[:])
        weigh_h(3)

        close = {}

        def closeness(step):
            tile = sb([P, T2], F32, "close%d" % step, AT_CLOSE[step])
            nc.scalar.activation(tile[:], pages[step % 2][:], ACT.Exp, scale=-1.0)
            close[step] = tile

        closeness(0)
        closeness(1)
        pairs0 = sb([P, 2, 2 * T2], BF16, "pairs0", AT_PAIRS0)

        def weigh_z0(step):
            u, e = divmod(step, 2)
            dst = pairs0[:, u, :].rearrange("p (c e) -> p c e", e=2)[:, :, e]
            nc.gpsimd.tensor_tensor(dst, close[step][:], bed[step][:], MULT)

        weigh_z0(0)
        place(2)
        for step in range(4, 8):
            distances(step)
        weigh_h(4)
        load_bed(1)
        place(3)
        for step in range(5, 7):
            weigh_h(step)
        weigh_z0(1)
        weigh_h(7)
        for step in range(2, 4):
            closeness(step)
            weigh_z0(step)
            place(step + 2)

        pairs1 = sb([P, 4 * T2], BF16, "pairs1", AT_PAIRS1)
        pairs1_view = pairs1[:].rearrange("p (k u c e) -> p k u c e", k=CHUNKS, u=2, e=2)
        for step in range(4, 6):
            closeness(step)
            nc.gpsimd.tensor_tensor(
                pairs1_view[:, :, 0, :, step % 2],
                close[step][:].rearrange("p (k c) -> p k c", k=CHUNKS),
                bed[step][:].rearrange("p (k c) -> p k c", k=CHUNKS), MULT,
            )
            place(step + 2)

        def weave(dst, src):
            nc.scalar.copy(dst.bitcast(U32).rearrange("p (c u) -> p c u", u=2), src.rearrange("p u c -> p c u"))

        z0 = sb([P, 4 * T2], BF16, "z0", AT_Z0)
        for k in range(CHUNKS):
            weave(z0[:, 4 * BANK * k:4 * BANK * (k + 1)], pairs0[:].bitcast(U32)[:, :, BANK * k:BANK * (k + 1)])

        close67 = sb([P, 2, T2], F32, "close67", AT_CLOSE67)
        nc.scalar.activation(close67[:, 0, :], pages[0][:], ACT.Exp, scale=-1.0)
        for k in range(CHUNKS):
            cols = slice(k * BANK, (k + 1) * BANK)
            nc.scalar.activation(close67[:, 1, cols], pages[1][:, cols], ACT.Exp, scale=-1.0)

        z_codes = {}
        z_sc = [sb([P, T2], U8, "z_sc%d" % b, AT_ZSC[b]) for b in range(PASS2)]
        sums = {}

        def feature_pass(n, k, b):
            first = (n, k) not in sums
            if first:
                sums[(n, k)] = bank(CHUNKS * min(n, 1) + k)
            cols = slice(k * BANK, (k + 1) * BANK)
            nc.tensor.matmul_mx(
                sums[(n, k)][:],
                lhsT=w4_sb[:, b, 2 * n * P:2 * (n + 1) * P].bitcast(FP4X4),
                lhsT_scale=w4_sc[:, b, n * P:(n + 1) * P],
                rhs=z_codes[(b, k)].bitcast(FP8X4),
                rhs_scale=z_sc[b][:, cols],
                start=first, stop=not first,
            )

        def quantise_z(b, k0, k1, src):
            cols = slice(k0 * BANK, k1 * BANK)
            codes = sb([P, (k1 - k0) * BANK], U32, "z_codes%d_%d" % (b, k0), AT_ZCODES[b][k0])
            quantise(codes[:], z_sc[b][:, cols], src)
            for k in range(k0, k1):
                z_codes[(b, k)] = codes[:, (k - k0) * BANK:(k - k0 + 1) * BANK]
            for n in range(2):
                for k in range(k0, k1):
                    feature_pass(n, k, b)

        z1 = []
        for k in range(CHUNKS):
            if k == 0:
                quantise_z(0, 0, 2, z0[:, 0:8 * BANK])
            cols = slice(k * BANK, (k + 1) * BANK)
            at = (2 * k + 1) * 2 * BANK
            nc.vector.tensor_tensor(
                pairs1[:, at:at + 2 * BANK].rearrange("p (c i e) -> p c e i", i=4, e=2),
                close67[:, :, cols].rearrange("p e (c i) -> p c e i", i=4),
                bed67[:, :, cols].rearrange("p e (c i) -> p c e i", i=4),
                MULT,
            )
            z1.append(sb([P, 4 * BANK], BF16, "z1_%d" % k, AT_Z1 + 4 * k))
            words = pairs1[:, 4 * BANK * k:4 * BANK * (k + 1)].bitcast(U32)
            weave(z1[k][:], words.rearrange("p (u c) -> p u c", u=2))
        for k in range(CHUNKS):
            if k == 2:
                quantise_z(0, 2, 4, z0[:, 8 * BANK:16 * BANK])
            quantise_z(1, k, k + 1, z1[k][:])

        ys = [sb([P, T2], F32, "y%d" % n, AT_Y[n]) for n in range(NT)]
        for n in range(NT):
            for k in range(CHUNKS):
                if n == 2:
                    for b in range(PASS2):
                        feature_pass(n, k, b)
                copy = nc.vector.tensor_copy if (n, k) == (0, CHUNKS - 1) else nc.scalar.copy
                copy(ys[n][:, k * BANK:(k + 1) * BANK], sums[(n, k)][:])

        picked = []
        for n in range(NT):
            x = sb([P, PK], F32, "x%d" % n, AT_X[n])
            nc.vector.tensor_copy(x[:], ys[n][:].indirect(idx3[:]))
            picked.append(x)
        for n in range(NT):
            score = sb([P, PK], F32, "score%d" % n, AT_SCORE[n])
            desk = desks[n % 2]
            for lo, width in parts if n == 0 else [(0, PK)]:
                cols = slice(lo, lo + width)
                square = sb([P, width], F32, "square%d_%d" % (n, lo), AT_SQUARE)
                nc.scalar.activation(square[:], picked[n][:, cols], ACT.Square)
                nc.scalar.activation(score[:, cols], square[:], ACT.Ln, bias=1.0)
                nc.vector.tensor_tensor(
                    desk[:].indirect(idx4[:, lo // 16:(lo + width) // 16]), score[:, cols], wgo_sb[:, cols], MULT
                )
            nc.sync.dma_start(out[n * P:(n + 1) * P, :], desk[:])
